import numpy as np
import ml_dtypes


def mxq(x, axis, fmt="e4m3"):
    dtype, down = {"e4m3": (ml_dtypes.float8_e4m3fn, 7), "e5m2": (ml_dtypes.float8_e5m2, 14)}[fmt]
    v = np.moveaxis(np.asarray(x, np.float32).astype(ml_dtypes.bfloat16).astype(np.float64), axis, -1)
    blocks = v.reshape(v.shape[:-1] + (-1, 32))
    amax = np.abs(blocks).max(-1, keepdims=True)
    byte = np.maximum(np.where(amax > 0, np.frexp(amax)[1] - 1 + 127, 0) - down, 1)
    scale = np.exp2(byte - 127.0)
    codes = (blocks / scale).astype(np.float32).astype(dtype).astype(np.float64)
    return np.moveaxis((codes * scale).reshape(v.shape), -1, axis)


WIDE = False


def mx_kscale(k):
    if not WIDE:
        return np.ones(k)
    levels = np.array([10, -10, 5, -5, 0])
    if k % 512:
        return np.exp2(np.random.permutation(np.resize(levels, k // 32))).repeat(32)
    a = np.empty((k // 512, 16))
    for p in range(k // 512):
        a[p, :8] = np.random.permutation(np.resize(levels, 8))
        for g in range(8):
            far = levels[np.abs(levels - a[p, g]) >= 10]
            a[p, g + 8] = far[np.random.randint(len(far))]
    return np.exp2(a.ravel()).repeat(32)


def f64(x):
    return np.asarray(x).astype(np.float64)


def striped(idx):
    return np.tile(idx.reshape(-1, 16).T, (8, 1)).astype(np.uint16)


def unstriped(offs):
    return offs[:16].T.reshape(-1).astype(np.int64)


def pack_weight(w):
    k, n = w.shape
    w = f64(np.asarray(w, np.float32).astype(ml_dtypes.bfloat16)).reshape(k // 32, 32, n)
    amax = np.abs(w).max(1)
    byte = np.clip(np.where(amax > 0, np.frexp(amax)[1] - 1 + 127 - 7, 1), 1, 254)
    scaled = (w * np.exp2(127.0 - byte)[:, None, :]).reshape(k, n).astype(np.float32)
    words = np.ascontiguousarray(scaled.reshape(k // 512, 128, 4, n).transpose(0, 1, 3, 2)).astype(ml_dtypes.float8_e4m3fn).view(np.uint8)
    return words, np.ascontiguousarray(byte.astype(np.uint8).reshape(k // 512, 16, n))


def unpack_weight(words, scales):
    g, p, n, _ = words.shape
    vals = np.ascontiguousarray(words).view(ml_dtypes.float8_e4m3fn).astype(np.float64) * np.repeat(np.exp2(scales.astype(np.float64) - 127.0), 8, axis=1)[..., None]
    return vals.transpose(0, 1, 3, 2).reshape(g * 512, n)


K, T, S, H, D, V, W, U, G = 1024, 2048, 512, 512, 4, 256, 2048, 1024, 1024


def setup_inputs():
    n = np.random.standard_normal
    s = mx_kscale(K)[:, None]
    u = mx_kscale(H)
    packed_xT = pack_weight(n((K, T)) * s)
    packed_eT = pack_weight(n((H, W)) / np.sqrt(H) / u[:, None])
    packed_dT = pack_weight(n((H, G)) / np.sqrt(H) / u[:, None])
    return {
        "x_words": packed_xT[0],
        "x_scales": packed_xT[1],
        "w1": (n((K, H)) / np.sqrt(K) / s * u).astype(np.float32),
        "e_words": packed_eT[0],
        "e_scales": packed_eT[1],
        "d_words": packed_dT[0],
        "d_scales": packed_dT[1],
        "offs": striped(np.random.permutation(T)[:S]),
        "user": striped(np.random.permutation(G)[:V]),
        "shown": striped(np.random.permutation(W)[:U]),
    }


def reference(x_words, x_scales, w1, e_words, e_scales, d_words, d_scales, offs, user, shown):
    xq = unpack_weight(x_words, x_scales)[:, unstriped(offs)]
    h = mxq(f64(w1), 0, "e4m3").T @ xq
    hq = mxq(h, 0, "e4m3")
    d_user = unpack_weight(d_words, d_scales)[:, unstriped(user)]
    y = hq.T @ d_user
    e_shown = unpack_weight(e_words, e_scales)[:, unstriped(shown)]
    z = hq.T @ e_shown
    near = z.reshape(len(z), -1, D).max(axis=2)
    return 0.7 * y - (0.3 * near)

@@ -1,0 +1,181 @@
+from contextlib import ExitStack
+
+import concourse.mybir as mybir
+
+K, T, S, H, D, V, W, U, G = 1024, 2048, 512, 512, 4, 256, 2048, 1024, 1024
+FLOPS = 2 * H * S * (K + V + U)
+
+F32 = mybir.dt.float32
+BF16 = mybir.dt.bfloat16
+I32 = mybir.dt.int32
+U32 = mybir.dt.uint32
+U16 = mybir.dt.uint16
+U8 = mybir.dt.uint8
+FP8X4 = mybir.dt.float8_e4m3fn_x4
+ALU = mybir.AluOpType
+COPY = mybir.ActivationFunctionType.Copy
+
+P = 128
+PACK = 4
+BANK = 512
+E_ROW = 8
+D_ROW = 12
+
+
+def tile_picked_ymmr_mmr_p_kernel(
+    tc, x_words, x_scales, w1, e_words, e_scales, d_words, d_scales, offs, user, shown, out
+):
+    nc = tc.nc
+    with ExitStack() as ctx:
+        keep = ctx.enter_context(tc.tile_pool(name="keep", bufs=1))
+        ring = ctx.enter_context(tc.tile_pool(name="ring", bufs=2))
+        psum = ctx.enter_context(tc.psum_pool(name="psum", bufs=2))
+        zpool = ctx.enter_context(tc.psum_pool(name="zpool", bufs=6))
+
+        def tile(shape, dtype, name, slot=None):
+            return keep.tile(shape, dtype, name=name, tag=slot or name, align_bytes=64)
+
+        def load_list(src, name):
+            t = keep.tile(list(src.shape), U16, name=name)
+            nc.sync.dma_start(t[:], src)
+            return t
+
+        def load_words(src, name):
+            t = tile([P, src.shape[1]], I32, name)
+            nc.sync.dma_start(t[:], src.rearrange("p n r -> p (n r)").bitcast(I32))
+            return t
+
+        def zeroed(width, name):
+            t = tile([P, width], U8, name)
+            nc.vector.memset(t[:].bitcast(I32), 0)
+            return t
+
+        def load_scales(queue, t, src, row):
+            rows = 4 * src.shape[0]
+            for q in range(4):
+                queue.dma_start(
+                    t[32 * q + row : 32 * q + row + rows, :].bitcast(I32),
+                    src[:, 4 * q : 4 * q + 4, :].bitcast(I32),
+                )
+
+        def load_w(o):
+            t = tile([P, PACK, H], F32, "w_raw%d" % o)
+            nc.sync.dma_start(t[:], w1[o * 512 : (o + 1) * 512, :].rearrange("(p j) c -> p j c", j=PACK))
+            return t
+
+        def gather(table, offsets, dtype, name, slot=None):
+            t = tile([P, 16 * offsets.shape[1]], dtype, name, slot)
+            nc.vector.tensor_copy(t[:], table[:].bitcast(dtype).indirect(offsets))
+            return t
+
+        def gather_bytes(table, offsets, name, slot=None):
+            t = tile([P, 16 * offsets.shape[1]], U8, name, slot)
+            nc.vector.tensor_copy(t[:], table[:].indirect(offsets))
+            return t
+
+        es_tab = zeroed(W, "es_tab")
+        xs_tab = zeroed(T, "xs_tab")
+        ds_tab = zeroed(G, "ds_tab")
+
+        w_raw = [load_w(0)]
+        shown_t = load_list(shown, "shown_t")
+        load_scales(nc.sync, es_tab, e_scales, E_ROW)
+        w_raw.append(load_w(1))
+        offs_t = load_list(offs, "offs_t")
+        load_scales(nc.sync, xs_tab, x_scales, 0)
+        x_tab = [load_words(x_words[0], "x_tab0")]
+        user_t = load_list(user, "user_t")
+        load_scales(nc.sync, ds_tab, d_scales, D_ROW)
+        x_tab.append(load_words(x_words[1], "x_tab1"))
+        d_tab = load_words(d_words[0], "d_tab")
+        e_tab = load_words(e_words[0], "e_tab")
+
+        def quantise_w(o):
+            grouped = tile([P, PACK * H], BF16, "w_grouped%d" % o)
+            nc.scalar.copy(
+                grouped[:].rearrange("p (t m j) -> p m t j", t=4, j=PACK),
+                w_raw[o][:].rearrange("p j (m t) -> p m t j", t=4),
+            )
+            codes = tile([P, H], U32, "w_codes%d" % o)
+            scales = tile([P, H], U8, "w_scales%d" % o, "ds_tab" if o else None)
+            nc.vector.quantize_mx(codes[:].bitcast(FP8X4), scales[:], grouped[:])
+            return codes, scales
+
+        e_sc = gather_bytes(es_tab, shown_t[:], "e_sc")
+        x_sc = gather_bytes(xs_tab, offs_t[:], "x_sc")
+        wq = [quantise_w(0)]
+        x0 = gather(x_tab[0], offs_t[:], U32, "x0", "xs_tab")
+        warm = zpool.tile([P, BANK], F32, name="z")
+        for t in range(3):
+            ch = slice(t * P, (t + 1) * P)
+            nc.tensor.matmul_mx(
+                warm[:], lhsT=wq[0][0][:, ch].bitcast(FP8X4), lhsT_scale=wq[0][1][:, ch],
+                rhs=x0[:].bitcast(FP8X4), rhs_scale=x_sc[:], start=True, stop=True,
+            )
+        d_sc = gather_bytes(ds_tab, user_t[:], "d_sc", "x_tab0")
+        wq.append(quantise_w(1))
+        x1 = tile([P, S], U32, "x1", "w_grouped1")
+        for u in range(2):
+            nc.vector.tensor_copy(
+                x1[:, 256 * u : 256 * u + 256], x_tab[1][:].bitcast(U32).indirect(offs_t[:, 16 * u : 16 * u + 16])
+            )
+        d_codes = gather(d_tab, user_t[:], U32, "d_codes", "x_tab1")
+
+        def hidden(c):
+            cols = slice(c * P, (c + 1) * P)
+            acc = zpool.tile([P, PACK, P], F32, name="z")
+            for t in range(PACK):
+                ch = slice(t * P, (t + 1) * P)
+                for o in range(2):
+                    nc.tensor.matmul_mx(
+                        acc[:, t, :],
+                        lhsT=wq[o][0][:, ch].bitcast(FP8X4),
+                        lhsT_scale=wq[o][1][:, ch],
+                        rhs=(x0[:, cols] if o == 0 else x1[:, cols]).bitcast(FP8X4),
+                        rhs_scale=x_sc[4 * o : P, cols],
+                        start=(o == 0),
+                        stop=(o == 1),
+                    )
+            grouped = tile([P, P * PACK], BF16, "h_grouped%d" % c)
+            nc.scalar.copy(grouped[:].rearrange("p (s t) -> p s t", t=PACK), acc[:].rearrange("p t s -> p s t"))
+            codes = tile([P, P], U32, "h_codes%d" % c)
+            scales = tile([P, P], U8, "h_scales%d" % c)
+            nc.vector.quantize_mx(codes[:].bitcast(FP8X4), scales[:], grouped[:])
+            return codes, scales
+
+        hq = [hidden(c) for c in range(4)]
+        e_codes = [gather(e_tab, shown_t[:, 32 * b : 32 * b + 32], U32, "e_codes%d" % b, "h_grouped%d" % (2 * b + 1)) for b in range(2)]
+        ybank = [psum.tile([P, 2, V], F32, name="y") for u in range(2)]
+        for c in range(4):
+            nc.tensor.matmul_mx(
+                ybank[c // 2][:, c % 2, :], lhsT=hq[c][0][:].bitcast(FP8X4), lhsT_scale=hq[c][1][:],
+                rhs=d_codes[:].bitcast(FP8X4), rhs_scale=d_sc[D_ROW:P, :], start=True, stop=True,
+            )
+        pair = [tile([P, 2, V], F32, "pair%d" % c) for c in range(4)]
+
+        def seen(c, b):
+            codes, scales = hq[c]
+            cols = slice(b * BANK, (b + 1) * BANK)
+            users = slice(b * P, (b + 1) * P)
+            z = zpool.tile([P, BANK], F32, name="z")
+            nc.tensor.matmul_mx(
+                z[:], lhsT=codes[:].bitcast(FP8X4), lhsT_scale=scales[:],
+                rhs=e_codes[b][:].bitcast(FP8X4), rhs_scale=e_sc[E_ROW:P, cols], start=True, stop=True,
+            )
+            zd = z[:].rearrange("p (v d) -> p d v", d=D)
+            low = tile([P, 2, P], F32, "low%d_%d" % (c, b))
+            nc.scalar.activation(low[:], zd[:, 0:2, :], COPY, scale=-0.3)
+            nc.vector.scalar_tensor_tensor(pair[c][:, :, users], zd[:, 2:4, :], -0.3, low[:], ALU.mult, ALU.min)
+
+        def finish(c):
+            near = tile([P, V], F32, "near%d" % c)
+            nc.vector.tensor_tensor(near[:], pair[c][:, 0, :], pair[c][:, 1, :], ALU.min)
+            res = tile([P, V], F32, "res%d" % c)
+            nc.vector.scalar_tensor_tensor(res[:], ybank[c // 2][:, c % 2, :], 0.7, near[:], ALU.mult, ALU.add)
+            nc.sync.dma_start(out[c * P : (c + 1) * P, :], res[:])
+
+        for c in range(4):
+            seen(c, 0)
+        for c in range(4):
+            seen(c, 1)
+            finish(c)

@@ -87,39 +87,34 @@ def tile_picked_ymmr_mmr_p_kernel(
         user_t = load_list(user, "user_t")
         load_scales(nc.sync, ds_tab, d_scales, D_ROW)
         x_tab.append(load_words(x_words[1], "x_tab1"))
-        d_tab = load_words(d_words[0], "d_tab")
         e_tab = load_words(e_words[0], "e_tab")
+        d_tab = load_words(d_words[0], "d_tab")
 
         def quantise_w(o):
             grouped = tile([P, PACK * H], BF16, "w_grouped%d" % o)
             nc.scalar.copy(
-                grouped[:].rearrange("p (t m j) -> p m t j", t=4, j=PACK),
-                w_raw[o][:].rearrange("p j (m t) -> p m t j", t=4),
+                grouped[:].rearrange("p (t m j) -> p m j t", t=4, j=PACK),
+                w_raw[o][:].rearrange("p j (m t) -> p m j t", t=4),
             )
-            codes = tile([P, H], U32, "w_codes%d" % o)
-            scales = tile([P, H], U8, "w_scales%d" % o, "ds_tab" if o else None)
+            codes = tile([P, H], U32, "w_codes%d" % o, "xs_tab" if o else None)
+            scales = tile([P, H], U8, "w_scales%d" % o)
             nc.vector.quantize_mx(codes[:].bitcast(FP8X4), scales[:], grouped[:])
             return codes, scales
 
         e_sc = gather_bytes(es_tab, shown_t[:], "e_sc")
-        x_sc = gather_bytes(xs_tab, offs_t[:], "x_sc")
         wq = [quantise_w(0)]
-        x0 = gather(x_tab[0], offs_t[:], U32, "x0", "xs_tab")
-        warm = zpool.tile([P, BANK], F32, name="z")
-        for t in range(3):
-            ch = slice(t * P, (t + 1) * P)
-            nc.tensor.matmul_mx(
-                warm[:], lhsT=wq[0][0][:, ch].bitcast(FP8X4), lhsT_scale=wq[0][1][:, ch],
-                rhs=x0[:].bitcast(FP8X4), rhs_scale=x_sc[:], start=True, stop=True,
-            )
-        d_sc = gather_bytes(ds_tab, user_t[:], "d_sc", "x_tab0")
+        x_sc = gather_bytes(xs_tab, offs_t[:], "x_sc")
         wq.append(quantise_w(1))
-        x1 = tile([P, S], U32, "x1", "w_grouped1")
+        x0 = gather(x_tab[0], offs_t[:], U32, "x0")
+        d_sc = gather_bytes(ds_tab, user_t[:], "d_sc")
+        x1 = tile([P, S], U32, "x1")
         for u in range(2):
             nc.vector.tensor_copy(
                 x1[:, 256 * u : 256 * u + 256], x_tab[1][:].bitcast(U32).indirect(offs_t[:, 16 * u : 16 * u + 16])
             )
-        d_codes = gather(d_tab, user_t[:], U32, "d_codes", "x_tab1")
+        e_codes = gather(e_tab, shown_t[:], U32, "e_codes")
+
+        h_codes = tile([P, S], U32, "h_codes", "e_tab")
 
         def hidden(c):
             cols = slice(c * P, (c + 1) * P)
@@ -138,44 +133,40 @@ def tile_picked_ymmr_mmr_p_kernel(
                     )
             grouped = tile([P, P * PACK], BF16, "h_grouped%d" % c)
             nc.scalar.copy(grouped[:].rearrange("p (s t) -> p s t", t=PACK), acc[:].rearrange("p t s -> p s t"))
-            codes = tile([P, P], U32, "h_codes%d" % c)
+            codes = h_codes[:, cols]
             scales = tile([P, P], U8, "h_scales%d" % c)
-            nc.vector.quantize_mx(codes[:].bitcast(FP8X4), scales[:], grouped[:])
+            nc.vector.quantize_mx(codes.bitcast(FP8X4), scales[:], grouped[:])
             return codes, scales
 
         hq = [hidden(c) for c in range(4)]
-        e_codes = [gather(e_tab, shown_t[:, 32 * b : 32 * b + 32], U32, "e_codes%d" % b, "h_grouped%d" % (2 * b + 1)) for b in range(2)]
+        d_codes = gather(d_tab, user_t[:], U32, "d_codes")
         ybank = [psum.tile([P, 2, V], F32, name="y") for u in range(2)]
         for c in range(4):
             nc.tensor.matmul_mx(
-                ybank[c // 2][:, c % 2, :], lhsT=hq[c][0][:].bitcast(FP8X4), lhsT_scale=hq[c][1][:],
+                ybank[c // 2][:, c % 2, :], lhsT=hq[c][0].bitcast(FP8X4), lhsT_scale=hq[c][1][:],
                 rhs=d_codes[:].bitcast(FP8X4), rhs_scale=d_sc[D_ROW:P, :], start=True, stop=True,
             )
-        pair = [tile([P, 2, V], F32, "pair%d" % c) for c in range(4)]
+        pairs = tile([P, 4, 2, V], F32, "pairs")
 
-        def seen(c, b):
+        for c in range(4):
             codes, scales = hq[c]
-            cols = slice(b * BANK, (b + 1) * BANK)
-            users = slice(b * P, (b + 1) * P)
-            z = zpool.tile([P, BANK], F32, name="z")
-            nc.tensor.matmul_mx(
-                z[:], lhsT=codes[:].bitcast(FP8X4), lhsT_scale=scales[:],
-                rhs=e_codes[b][:].bitcast(FP8X4), rhs_scale=e_sc[E_ROW:P, cols], start=True, stop=True,
-            )
-            zd = z[:].rearrange("p (v d) -> p d v", d=D)
-            low = tile([P, 2, P], F32, "low%d_%d" % (c, b))
-            nc.scalar.activation(low[:], zd[:, 0:2, :], COPY, scale=-0.3)
-            nc.vector.scalar_tensor_tensor(pair[c][:, :, users], zd[:, 2:4, :], -0.3, low[:], ALU.mult, ALU.min)
-
-        def finish(c):
+            pair = pairs[:, c]
+            for b in range(2):
+                cols = slice(b * BANK, (b + 1) * BANK)
+                z = zpool.tile([P, BANK], F32, name="z")
+                nc.tensor.matmul_mx(
+                    z[:], lhsT=codes.bitcast(FP8X4), lhsT_scale=scales[:],
+                    rhs=e_codes[:, cols].bitcast(FP8X4), rhs_scale=e_sc[E_ROW:P, cols], start=True, stop=True,
+                )
+                zd = z[:].rearrange("p (v d) -> p d v", d=D)
+                low = tile([P, 2, P], F32, "low%d_%d" % (c, b))
+                nc.scalar.activation(low[:], zd[:, 0:2, :], COPY, scale=-0.3)
+                nc.vector.scalar_tensor_tensor(
+                    pair[:, :, b * P : (b + 1) * P], zd[:, 2:4, :], -0.3, low[:], ALU.mult, ALU.min
+                )
+            y = ybank[c // 2][:, c % 2, :]
             near = tile([P, V], F32, "near%d" % c)
-            nc.vector.tensor_tensor(near[:], pair[c][:, 0, :], pair[c][:, 1, :], ALU.min)
+            nc.vector.tensor_tensor(near[:], pair[:, 0, :], pair[:, 1, :], ALU.min)
             res = tile([P, V], F32, "res%d" % c)
-            nc.vector.scalar_tensor_tensor(res[:], ybank[c // 2][:, c % 2, :], 0.7, near[:], ALU.mult, ALU.add)
+            nc.vector.scalar_tensor_tensor(res[:], y, 0.7, near[:], ALU.mult, ALU.add)
             nc.sync.dma_start(out[c * P : (c + 1) * P, :], res[:])
-
-        for c in range(4):
-            seen(c, 0)
-        for c in range(4):
-            seen(c, 1)
-            finish(c)

@@ -93,10 +93,10 @@ def tile_picked_ymmr_mmr_p_kernel(
         def quantise_w(o):
             grouped = tile([P, PACK * H], BF16, "w_grouped%d" % o)
             nc.scalar.copy(
-                grouped[:].rearrange("p (t m j) -> p m j t", t=4, j=PACK),
-                w_raw[o][:].rearrange("p j (m t) -> p m j t", t=4),
+                grouped[:].rearrange("p (t m j) -> p m t j", t=4, j=PACK),
+                w_raw[o][:].rearrange("p j (m t) -> p m t j", t=4),
             )
-            codes = tile([P, H], U32, "w_codes%d" % o, "xs_tab" if o else None)
+            codes = tile([P, H], U32, "w_codes%d" % o, "ds_tab" if o else None)
             scales = tile([P, H], U8, "w_scales%d" % o)
             nc.vector.quantize_mx(codes[:].bitcast(FP8X4), scales[:], grouped[:])
             return codes, scales
@@ -104,9 +104,9 @@ def tile_picked_ymmr_mmr_p_kernel(
         e_sc = gather_bytes(es_tab, shown_t[:], "e_sc")
         wq = [quantise_w(0)]
         x_sc = gather_bytes(xs_tab, offs_t[:], "x_sc")
-        wq.append(quantise_w(1))
         x0 = gather(x_tab[0], offs_t[:], U32, "x0")
         d_sc = gather_bytes(ds_tab, user_t[:], "d_sc")
+        wq.append(quantise_w(1))
         x1 = tile([P, S], U32, "x1")
         for u in range(2):
             nc.vector.tensor_copy(

@@ -29,11 +29,14 @@ def tile_picked_ymmr_mmr_p_kernel(
     with ExitStack() as ctx:
         keep = ctx.enter_context(tc.tile_pool(name="keep", bufs=1))
         ring = ctx.enter_context(tc.tile_pool(name="ring", bufs=2))
+        reuse = ctx.enter_context(tc.tile_pool(name="reuse", bufs=1))
         psum = ctx.enter_context(tc.psum_pool(name="psum", bufs=2))
         zpool = ctx.enter_context(tc.psum_pool(name="zpool", bufs=6))
 
-        def tile(shape, dtype, name, slot=None):
-            return keep.tile(shape, dtype, name=name, tag=slot or name, align_bytes=64)
+        def tile(shape, dtype, name, at=None):
+            if at is None:
+                return keep.tile(shape, dtype, name=name, align_bytes=64)
+            return reuse.tile(shape, dtype, name=name, align_bytes=64, offset=at)
 
         def load_list(src, name):
             t = keep.tile(list(src.shape), U16, name=name)
@@ -74,7 +77,9 @@ def tile_picked_ymmr_mmr_p_kernel(
             return t
 
         es_tab = zeroed(W, "es_tab")
-        xs_tab = zeroed(T, "xs_tab")
+        xs_tab = tile([P, T], U8, "xs_tab", 4032)
+        nc.gpsimd.memset(xs_tab[:].bitcast(I32), 0)
+        load_scales(nc.gpsimd, xs_tab, x_scales, 0)
         ds_tab = zeroed(G, "ds_tab")
 
         w_raw = [load_w(0)]
@@ -82,7 +87,6 @@ def tile_picked_ymmr_mmr_p_kernel(
         load_scales(nc.sync, es_tab, e_scales, E_ROW)
         w_raw.append(load_w(1))
         offs_t = load_list(offs, "offs_t")
-        load_scales(nc.sync, xs_tab, x_scales, 0)
         x_tab = [load_words(x_words[0], "x_tab0")]
         user_t = load_list(user, "user_t")
         load_scales(nc.sync, ds_tab, d_scales, D_ROW)
@@ -96,25 +100,26 @@ def tile_picked_ymmr_mmr_p_kernel(
                 grouped[:].rearrange("p (t m j) -> p m t j", t=4, j=PACK),
                 w_raw[o][:].rearrange("p j (m t) -> p m t j", t=4),
             )
-            codes = tile([P, H], U32, "w_codes%d" % o, "ds_tab" if o else None)
-            scales = tile([P, H], U8, "w_scales%d" % o)
+            codes = tile([P, H], U32, "w_codes%d" % o)
+            scales = tile([P, H], U8, "w_scales%d" % o, 4352 if o else None)
             nc.vector.quantize_mx(codes[:].bitcast(FP8X4), scales[:], grouped[:])
             return codes, scales
 
         e_sc = gather_bytes(es_tab, shown_t[:], "e_sc")
         wq = [quantise_w(0)]
         x_sc = gather_bytes(xs_tab, offs_t[:], "x_sc")
-        x0 = gather(x_tab[0], offs_t[:], U32, "x0")
-        d_sc = gather_bytes(ds_tab, user_t[:], "d_sc")
+        x_codes = tile([P, 2 * S], U32, "x_codes", 5888)
+        nc.vector.tensor_copy(x_codes[:, 0:S], x_tab[0][:].bitcast(U32).indirect(offs_t[:]))
+        d_sc = gather_bytes(ds_tab, user_t[:], "d_sc", 4096)
         wq.append(quantise_w(1))
-        x1 = tile([P, S], U32, "x1")
         for u in range(2):
             nc.vector.tensor_copy(
-                x1[:, 256 * u : 256 * u + 256], x_tab[1][:].bitcast(U32).indirect(offs_t[:, 16 * u : 16 * u + 16])
+                x_codes[:, S + 256 * u : S + 256 * u + 256],
+                x_tab[1][:].bitcast(U32).indirect(offs_t[:, 16 * u : 16 * u + 16]),
             )
-        e_codes = gather(e_tab, shown_t[:], U32, "e_codes")
-
-        h_codes = tile([P, S], U32, "h_codes", "e_tab")
+        e_codes = gather(e_tab, shown_t[:], U32, "e_codes", 0)
+        d_codes = gather(d_tab, user_t[:], U32, "d_codes", 4864)
+        h_codes = keep.tile([P, S], U32, name="h_codes", tag="e_tab", align_bytes=64)
 
         def hidden(c):
             cols = slice(c * P, (c + 1) * P)
@@ -126,7 +131,7 @@ def tile_picked_ymmr_mmr_p_kernel(
                         acc[:, t, :],
                         lhsT=wq[o][0][:, ch].bitcast(FP8X4),
                         lhsT_scale=wq[o][1][:, ch],
-                        rhs=(x0[:, cols] if o == 0 else x1[:, cols]).bitcast(FP8X4),
+                        rhs=x_codes[:, o * S + c * P : o * S + (c + 1) * P].bitcast(FP8X4),
                         rhs_scale=x_sc[4 * o : P, cols],
                         start=(o == 0),
                         stop=(o == 1),
@@ -139,34 +144,34 @@ def tile_picked_ymmr_mmr_p_kernel(
             return codes, scales
 
         hq = [hidden(c) for c in range(4)]
-        d_codes = gather(d_tab, user_t[:], U32, "d_codes")
-        ybank = [psum.tile([P, 2, V], F32, name="y") for u in range(2)]
-        for c in range(4):
-            nc.tensor.matmul_mx(
-                ybank[c // 2][:, c % 2, :], lhsT=hq[c][0].bitcast(FP8X4), lhsT_scale=hq[c][1][:],
-                rhs=d_codes[:].bitcast(FP8X4), rhs_scale=d_sc[D_ROW:P, :], start=True, stop=True,
-            )
-        pairs = tile([P, 4, 2, V], F32, "pairs")
-
-        for c in range(4):
-            codes, scales = hq[c]
-            pair = pairs[:, c]
-            for b in range(2):
-                cols = slice(b * BANK, (b + 1) * BANK)
-                z = zpool.tile([P, BANK], F32, name="z")
+        for u in range(2):
+            chunks = (2 * u, 2 * u + 1)
+            pair = {}
+            for c in chunks:
+                codes, scales = hq[c]
+                pair[c] = tile([P, 2, V], F32, "pair%d" % c)
+                for b in range(2):
+                    cols = slice(b * BANK, (b + 1) * BANK)
+                    z = zpool.tile([P, BANK], F32, name="z")
+                    nc.tensor.matmul_mx(
+                        z[:], lhsT=codes.bitcast(FP8X4), lhsT_scale=scales[:],
+                        rhs=e_codes[:, cols].bitcast(FP8X4), rhs_scale=e_sc[E_ROW:P, cols], start=True, stop=True,
+                    )
+                    zd = z[:].rearrange("p (v d) -> p d v", d=D)
+                    low = tile([P, 2, P], F32, "low%d_%d" % (c, b))
+                    nc.scalar.activation(low[:], zd[:, 0:2, :], COPY, scale=-0.3)
+                    nc.vector.scalar_tensor_tensor(
+                        pair[c][:, :, b * P : (b + 1) * P], zd[:, 2:4, :], -0.3, low[:], ALU.mult, ALU.min
+                    )
+            y = psum.tile([P, 2, V], F32, name="y")
+            for c in chunks:
                 nc.tensor.matmul_mx(
-                    z[:], lhsT=codes.bitcast(FP8X4), lhsT_scale=scales[:],
-                    rhs=e_codes[:, cols].bitcast(FP8X4), rhs_scale=e_sc[E_ROW:P, cols], start=True, stop=True,
+                    y[:, c % 2, :], lhsT=hq[c][0].bitcast(FP8X4), lhsT_scale=hq[c][1][:],
+                    rhs=d_codes[:].bitcast(FP8X4), rhs_scale=d_sc[D_ROW:P, :], start=True, stop=True,
                 )
-                zd = z[:].rearrange("p (v d) -> p d v", d=D)
-                low = tile([P, 2, P], F32, "low%d_%d" % (c, b))
-                nc.scalar.activation(low[:], zd[:, 0:2, :], COPY, scale=-0.3)
-                nc.vector.scalar_tensor_tensor(
-                    pair[:, :, b * P : (b + 1) * P], zd[:, 2:4, :], -0.3, low[:], ALU.mult, ALU.min
-                )
-            y = ybank[c // 2][:, c % 2, :]
-            near = tile([P, V], F32, "near%d" % c)
-            nc.vector.tensor_tensor(near[:], pair[:, 0, :], pair[:, 1, :], ALU.min)
-            res = tile([P, V], F32, "res%d" % c)
-            nc.vector.scalar_tensor_tensor(res[:], y, 0.7, near[:], ALU.mult, ALU.add)
-            nc.sync.dma_start(out[c * P : (c + 1) * P, :], res[:])
+            for c in chunks:
+                near = tile([P, V], F32, "near%d" % c)
+                nc.vector.tensor_tensor(near[:], pair[c][:, 0, :], pair[c][:, 1, :], ALU.min)
+                res = tile([P, V], F32, "res%d" % c)
+                nc.vector.scalar_tensor_tensor(res[:], y[:, c % 2, :], 0.7, near[:], ALU.mult, ALU.add)
+                nc.sync.dma_start(out[c * P : (c + 1) * P, :], res[:])

@@ -53,9 +53,9 @@ def tile_picked_ymmr_mmr_p_kernel(
             nc.vector.memset(t[:].bitcast(I32), 0)
             return t
 
-        def load_scales(queue, t, src, row):
+        def load_scales(queue, t, src, row, quadrants=range(4)):
             rows = 4 * src.shape[0]
-            for q in range(4):
+            for q in quadrants:
                 queue.dma_start(
                     t[32 * q + row : 32 * q + row + rows, :].bitcast(I32),
                     src[:, 4 * q : 4 * q + 4, :].bitcast(I32),
@@ -79,7 +79,7 @@ def tile_picked_ymmr_mmr_p_kernel(
         es_tab = zeroed(W, "es_tab")
         xs_tab = tile([P, T], U8, "xs_tab", 4032)
         nc.gpsimd.memset(xs_tab[:].bitcast(I32), 0)
-        load_scales(nc.gpsimd, xs_tab, x_scales, 0)
+        load_scales(nc.gpsimd, xs_tab, x_scales, 0, (0, 2))
         ds_tab = zeroed(G, "ds_tab")
 
         w_raw = [load_w(0)]
@@ -87,6 +87,7 @@ def tile_picked_ymmr_mmr_p_kernel(
         load_scales(nc.sync, es_tab, e_scales, E_ROW)
         w_raw.append(load_w(1))
         offs_t = load_list(offs, "offs_t")
+        load_scales(nc.sync, xs_tab, x_scales, 0, (1, 3))
         x_tab = [load_words(x_words[0], "x_tab0")]
         user_t = load_list(user, "user_t")
         load_scales(nc.sync, ds_tab, d_scales, D_ROW)
@@ -112,11 +113,7 @@ def tile_picked_ymmr_mmr_p_kernel(
         nc.vector.tensor_copy(x_codes[:, 0:S], x_tab[0][:].bitcast(U32).indirect(offs_t[:]))
         d_sc = gather_bytes(ds_tab, user_t[:], "d_sc", 4096)
         wq.append(quantise_w(1))
-        for u in range(2):
-            nc.vector.tensor_copy(
-                x_codes[:, S + 256 * u : S + 256 * u + 256],
-                x_tab[1][:].bitcast(U32).indirect(offs_t[:, 16 * u : 16 * u + 16]),
-            )
+        nc.vector.tensor_copy(x_codes[:, S : 2 * S], x_tab[1][:].bitcast(U32).indirect(offs_t[:]))
         e_codes = gather(e_tab, shown_t[:], U32, "e_codes", 0)
         d_codes = gather(d_tab, user_t[:], U32, "d_codes", 4864)
         h_codes = keep.tile([P, S], U32, name="h_codes", tag="e_tab", align_bytes=64)

@@ -61,6 +61,10 @@ def tile_picked_ymmr_mmr_p_kernel(
                     src[:, 4 * q : 4 * q + 4, :].bitcast(I32),
                 )
 
+        def load_scale_rows(t, src, row):
+            for r in range(4):
+                nc.sync.dma_start(t[row + r : P : 32, :].bitcast(I32), src[0, r:16:4, :].bitcast(I32))
+
         def load_w(o):
             t = tile([P, PACK, H], F32, "w_raw%d" % o)
             nc.sync.dma_start(t[:], w1[o * 512 : (o + 1) * 512, :].rearrange("(p j) c -> p j c", j=PACK))
@@ -84,13 +88,13 @@ def tile_picked_ymmr_mmr_p_kernel(
 
         w_raw = [load_w(0)]
         shown_t = load_list(shown, "shown_t")
-        load_scales(nc.sync, es_tab, e_scales, E_ROW)
+        load_scale_rows(es_tab, e_scales, E_ROW)
         w_raw.append(load_w(1))
         offs_t = load_list(offs, "offs_t")
         load_scales(nc.sync, xs_tab, x_scales, 0, (1, 3))
         x_tab = [load_words(x_words[0], "x_tab0")]
         user_t = load_list(user, "user_t")
-        load_scales(nc.sync, ds_tab, d_scales, D_ROW)
+        load_scale_rows(ds_tab, d_scales, D_ROW)
         x_tab.append(load_words(x_words[1], "x_tab1"))
         e_tab = load_words(e_words[0], "e_tab")
         d_tab = load_words(d_words[0], "d_tab")

@@ -20,6 +20,7 @@ PACK = 4
 BANK = 512
 E_ROW = 8
 D_ROW = 12
+XS_AT = 4 * W + 512
 
 
 def tile_picked_ymmr_mmr_p_kernel(
@@ -28,47 +29,43 @@ def tile_picked_ymmr_mmr_p_kernel(
     nc = tc.nc
     with ExitStack() as ctx:
         keep = ctx.enter_context(tc.tile_pool(name="keep", bufs=1))
-        ring = ctx.enter_context(tc.tile_pool(name="ring", bufs=2))
         reuse = ctx.enter_context(tc.tile_pool(name="reuse", bufs=1))
         psum = ctx.enter_context(tc.psum_pool(name="psum", bufs=2))
         zpool = ctx.enter_context(tc.psum_pool(name="zpool", bufs=6))
 
-        def tile(shape, dtype, name, at=None):
-            if at is None:
-                return keep.tile(shape, dtype, name=name, align_bytes=64)
-            return reuse.tile(shape, dtype, name=name, align_bytes=64, offset=at)
+        def tile(shape, dtype, name, slot=None):
+            if isinstance(slot, int):
+                return reuse.tile(shape, dtype, name=name, align_bytes=64, offset=slot)
+            return keep.tile(shape, dtype, name=name, tag=slot or name, align_bytes=64)
 
         def load_list(src, name):
             t = keep.tile(list(src.shape), U16, name=name)
             nc.sync.dma_start(t[:], src)
             return t
 
-        def load_words(src, name):
-            t = tile([P, src.shape[1]], I32, name)
+        def load_words(src, name, slot=None):
+            t = tile([P, src.shape[1]], I32, name, slot)
             nc.sync.dma_start(t[:], src.rearrange("p n r -> p (n r)").bitcast(I32))
             return t
 
-        def zeroed(width, name):
-            t = tile([P, width], U8, name)
-            nc.vector.memset(t[:].bitcast(I32), 0)
+        def zeroed(engine, width, name, slot=None):
+            t = tile([P, width], U8, name, slot)
+            engine.memset(t[:].bitcast(I32), 0)
             return t
 
-        def load_scales(queue, t, src, row, quadrants=range(4)):
-            rows = 4 * src.shape[0]
-            for q in quadrants:
-                queue.dma_start(
-                    t[32 * q + row : 32 * q + row + rows, :].bitcast(I32),
-                    src[:, 4 * q : 4 * q + 4, :].bitcast(I32),
-                )
+        def load_quadrant(queue, t, src, q):
+            queue.dma_start(
+                t[32 * q : 32 * q + 4 * src.shape[0], :].bitcast(I32),
+                src[:, 4 * q : 4 * q + 4, :].bitcast(I32),
+            )
 
         def load_scale_rows(t, src, row):
             for r in range(4):
                 nc.sync.dma_start(t[row + r : P : 32, :].bitcast(I32), src[0, r:16:4, :].bitcast(I32))
 
-        def load_w(o):
-            t = tile([P, PACK, H], F32, "w_raw%d" % o)
-            nc.sync.dma_start(t[:], w1[o * 512 : (o + 1) * 512, :].rearrange("(p j) c -> p j c", j=PACK))
-            return t
+        def load_w(o, j0, j1):
+            rows = w1[o * 512 : (o + 1) * 512, :].rearrange("(p j) c -> p j c", j=PACK)
+            nc.sync.dma_start(w_raw[o][:, j0:j1, :], rows[:, j0:j1, :])
 
         def gather(table, offsets, dtype, name, slot=None):
             t = tile([P, 16 * offsets.shape[1]], dtype, name, slot)
@@ -80,47 +77,54 @@ def tile_picked_ymmr_mmr_p_kernel(
             nc.vector.tensor_copy(t[:], table[:].indirect(offsets))
             return t
 
-        es_tab = zeroed(W, "es_tab")
-        xs_tab = tile([P, T], U8, "xs_tab", 4032)
-        nc.gpsimd.memset(xs_tab[:].bitcast(I32), 0)
-        load_scales(nc.gpsimd, xs_tab, x_scales, 0, (0, 2))
-        ds_tab = zeroed(G, "ds_tab")
+        es_tab = zeroed(nc.vector, W, "es_tab")
+        xs_tab = zeroed(nc.gpsimd, T, "xs_tab", XS_AT)
+        for q in (0, 2):
+            load_quadrant(nc.gpsimd, xs_tab, x_scales, q)
+        ds_tab = zeroed(nc.vector, G, "ds_tab")
+        warm = tile([P, 2], F32, "warm")
+        nc.gpsimd.memset(warm[:, 0:1], 0.0)
+        nc.scalar.activation(warm[:, 1:2], warm[:, 0:1], COPY)
 
-        w_raw = [load_w(0)]
+        w_raw = [tile([P, PACK, H], F32, "w_raw%d" % o) for o in range(2)]
+        load_w(0, 0, 2)
         shown_t = load_list(shown, "shown_t")
         load_scale_rows(es_tab, e_scales, E_ROW)
-        w_raw.append(load_w(1))
+        load_w(0, 2, PACK)
+        load_w(1, 0, PACK)
         offs_t = load_list(offs, "offs_t")
-        load_scales(nc.sync, xs_tab, x_scales, 0, (1, 3))
+        for q in (1, 3):
+            load_quadrant(nc.sync, xs_tab, x_scales, q)
         x_tab = [load_words(x_words[0], "x_tab0")]
         user_t = load_list(user, "user_t")
-        load_scale_rows(ds_tab, d_scales, D_ROW)
         x_tab.append(load_words(x_words[1], "x_tab1"))
-        e_tab = load_words(e_words[0], "e_tab")
+        load_scale_rows(ds_tab, d_scales, D_ROW)
+        e_tab = load_words(e_words[0], "e_tab", 0)
         d_tab = load_words(d_words[0], "d_tab")
 
-        def quantise_w(o):
+        def quantise_w(o, slot):
             grouped = tile([P, PACK * H], BF16, "w_grouped%d" % o)
             nc.scalar.copy(
                 grouped[:].rearrange("p (t m j) -> p m t j", t=4, j=PACK),
                 w_raw[o][:].rearrange("p j (m t) -> p m t j", t=4),
             )
             codes = tile([P, H], U32, "w_codes%d" % o)
-            scales = tile([P, H], U8, "w_scales%d" % o, 4352 if o else None)
+            scales = tile([P, H], U8, "w_scales%d" % o, slot)
             nc.vector.quantize_mx(codes[:].bitcast(FP8X4), scales[:], grouped[:])
             return codes, scales
 
         e_sc = gather_bytes(es_tab, shown_t[:], "e_sc")
-        wq = [quantise_w(0)]
+        wq = [quantise_w(0, None)]
         x_sc = gather_bytes(xs_tab, offs_t[:], "x_sc")
-        x_codes = tile([P, 2 * S], U32, "x_codes", 5888)
-        nc.vector.tensor_copy(x_codes[:, 0:S], x_tab[0][:].bitcast(U32).indirect(offs_t[:]))
-        d_sc = gather_bytes(ds_tab, user_t[:], "d_sc", 4096)
-        wq.append(quantise_w(1))
-        nc.vector.tensor_copy(x_codes[:, S : 2 * S], x_tab[1][:].bitcast(U32).indirect(offs_t[:]))
-        e_codes = gather(e_tab, shown_t[:], U32, "e_codes", 0)
-        d_codes = gather(d_tab, user_t[:], U32, "d_codes", 4864)
-        h_codes = keep.tile([P, S], U32, name="h_codes", tag="e_tab", align_bytes=64)
+        x_codes = [gather(x_tab[0], offs_t[:], U32, "x_codes0", XS_AT + 64 + V)]
+        wq.append(quantise_w(1, XS_AT + 64 - H))
+        x_codes.append(gather(x_tab[1], offs_t[:], U32, "x_codes1"))
+        d_sc = gather_bytes(ds_tab, user_t[:], "d_sc", XS_AT + 64)
+        e_codes = gather(e_tab, shown_t[:], U32, "e_codes", "x_tab1")
+        h_codes = tile([P, S], U32, "h_codes", 0)
+
+        h_grouped = tile([P, S, PACK], BF16, "h_grouped")
+        h_scales = tile([P, S], U8, "h_scales")
 
         def hidden(c):
             cols = slice(c * P, (c + 1) * P)
@@ -132,47 +136,74 @@ def tile_picked_ymmr_mmr_p_kernel(
                         acc[:, t, :],
                         lhsT=wq[o][0][:, ch].bitcast(FP8X4),
                         lhsT_scale=wq[o][1][:, ch],
-                        rhs=x_codes[:, o * S + c * P : o * S + (c + 1) * P].bitcast(FP8X4),
+                        rhs=x_codes[o][:, cols].bitcast(FP8X4),
                         rhs_scale=x_sc[4 * o : P, cols],
                         start=(o == 0),
                         stop=(o == 1),
                     )
-            grouped = tile([P, P * PACK], BF16, "h_grouped%d" % c)
-            nc.scalar.copy(grouped[:].rearrange("p (s t) -> p s t", t=PACK), acc[:].rearrange("p t s -> p s t"))
-            codes = h_codes[:, cols]
-            scales = tile([P, P], U8, "h_scales%d" % c)
-            nc.vector.quantize_mx(codes.bitcast(FP8X4), scales[:], grouped[:])
-            return codes, scales
+            nc.scalar.copy(h_grouped[:, cols, :], acc[:].rearrange("p t s -> p s t"))
 
-        hq = [hidden(c) for c in range(4)]
+        for c in range(4):
+            hidden(c)
         for u in range(2):
-            chunks = (2 * u, 2 * u + 1)
-            pair = {}
-            for c in chunks:
-                codes, scales = hq[c]
-                pair[c] = tile([P, 2, V], F32, "pair%d" % c)
-                for b in range(2):
-                    cols = slice(b * BANK, (b + 1) * BANK)
-                    z = zpool.tile([P, BANK], F32, name="z")
-                    nc.tensor.matmul_mx(
-                        z[:], lhsT=codes.bitcast(FP8X4), lhsT_scale=scales[:],
-                        rhs=e_codes[:, cols].bitcast(FP8X4), rhs_scale=e_sc[E_ROW:P, cols], start=True, stop=True,
-                    )
-                    zd = z[:].rearrange("p (v d) -> p d v", d=D)
-                    low = tile([P, 2, P], F32, "low%d_%d" % (c, b))
-                    nc.scalar.activation(low[:], zd[:, 0:2, :], COPY, scale=-0.3)
-                    nc.vector.scalar_tensor_tensor(
-                        pair[c][:, :, b * P : (b + 1) * P], zd[:, 2:4, :], -0.3, low[:], ALU.mult, ALU.min
-                    )
-            y = psum.tile([P, 2, V], F32, name="y")
-            for c in chunks:
+            cols = slice(u * 2 * P, (u + 1) * 2 * P)
+            nc.vector.quantize_mx(
+                h_codes[:, cols].bitcast(FP8X4), h_scales[:, cols], h_grouped[:, cols, :].rearrange("p s t -> p (s t)")
+            )
+        hq = [(h_codes[:, c * P : (c + 1) * P], h_scales[:, c * P : (c + 1) * P]) for c in range(4)]
+        d_codes = gather(d_tab, user_t[:], U32, "d_codes", 4 * S)
+        pair = tile([P, 4, V, 2], F32, "pair")
+        near = tile([P, 4, V], F32, "near")
+        res = tile([P, 4, V], F32, "res")
+        y = [psum.tile([P, 2, V], F32, name="y") for u in range(2)]
+
+        def seen(c):
+            codes, scales = hq[c]
+            for b in range(2):
+                cols = slice(b * BANK, (b + 1) * BANK)
+                z = zpool.tile([P, BANK], F32, name="z")
                 nc.tensor.matmul_mx(
-                    y[:, c % 2, :], lhsT=hq[c][0].bitcast(FP8X4), lhsT_scale=hq[c][1][:],
-                    rhs=d_codes[:].bitcast(FP8X4), rhs_scale=d_sc[D_ROW:P, :], start=True, stop=True,
+                    z[:], lhsT=codes.bitcast(FP8X4), lhsT_scale=scales,
+                    rhs=e_codes[:, cols].bitcast(FP8X4), rhs_scale=e_sc[E_ROW:P, cols], start=True, stop=True,
                 )
-            for c in chunks:
-                near = tile([P, V], F32, "near%d" % c)
-                nc.vector.tensor_tensor(near[:], pair[c][:, 0, :], pair[c][:, 1, :], ALU.min)
-                res = tile([P, V], F32, "res%d" % c)
-                nc.vector.scalar_tensor_tensor(res[:], y[:, c % 2, :], 0.7, near[:], ALU.mult, ALU.add)
-                nc.sync.dma_start(out[c * P : (c + 1) * P, :], res[:])
+                zd = z[:].rearrange("p (v d) -> p v d", d=D)
+                low = tile([P, P, 2], F32, "low%d_%d" % (c, b))
+                nc.scalar.activation(low[:], zd[:, :, 0:2], COPY, scale=-0.3)
+                nc.vector.scalar_tensor_tensor(
+                    pair[:, c, b * P : (b + 1) * P, :], zd[:, :, 2:4], -0.3, low[:], ALU.mult, ALU.min
+                )
+
+        def intent(c):
+            nc.tensor.matmul_mx(
+                y[c // 2][:, c % 2, :], lhsT=hq[c][0].bitcast(FP8X4), lhsT_scale=hq[c][1],
+                rhs=d_codes[:].bitcast(FP8X4), rhs_scale=d_sc[D_ROW:P, :], start=True, stop=True,
+            )
+
+        def nearest(c0, c1):
+            nc.vector.tensor_tensor(near[:, c0:c1, :], pair[:, c0:c1, :, 0], pair[:, c0:c1, :, 1], ALU.min)
+
+        def score(c0, c1):
+            nc.vector.scalar_tensor_tensor(
+                res[:, c0:c1, :], y[c0 // 2][:, c0 % 2 : c0 % 2 + c1 - c0, :], 0.7, near[:, c0:c1, :], ALU.mult, ALU.add
+            )
+            store(c0, c1)
+
+        def store(c0, c1):
+            nc.sync.dma_start(out[c0 * P : c1 * P, :].rearrange("(c p) v -> p c v", p=P), res[:, c0:c1, :])
+
+        seen(0)
+        seen(1)
+        intent(0)
+        intent(1)
+        nearest(0, 1)
+        nearest(1, 2)
+        seen(2)
+        score(0, 1)
+        score(1, 2)
+        seen(3)
+        intent(2)
+        intent(3)
+        nearest(2, 3)
+        nearest(3, 4)
+        score(2, 3)
+        score(3, 4)

@@ -91,14 +91,13 @@ def tile_picked_ymmr_mmr_p_kernel(
         shown_t = load_list(shown, "shown_t")
         load_scale_rows(es_tab, e_scales, E_ROW)
         load_w(0, 2, PACK)
-        load_w(1, 0, PACK)
         offs_t = load_list(offs, "offs_t")
         for q in (1, 3):
             load_quadrant(nc.sync, xs_tab, x_scales, q)
-        x_tab = [load_words(x_words[0], "x_tab0")]
+        load_w(1, 0, PACK)
         user_t = load_list(user, "user_t")
-        x_tab.append(load_words(x_words[1], "x_tab1"))
         load_scale_rows(ds_tab, d_scales, D_ROW)
+        x_tab = [load_words(x_words[o], "x_tab%d" % o) for o in range(2)]
         e_tab = load_words(e_words[0], "e_tab", 0)
         d_tab = load_words(d_words[0], "d_tab")
 
@@ -114,12 +113,12 @@ def tile_picked_ymmr_mmr_p_kernel(
             return codes, scales
 
         e_sc = gather_bytes(es_tab, shown_t[:], "e_sc")
-        wq = [quantise_w(0, None)]
         x_sc = gather_bytes(xs_tab, offs_t[:], "x_sc")
-        x_codes = [gather(x_tab[0], offs_t[:], U32, "x_codes0", XS_AT + 64 + V)]
-        wq.append(quantise_w(1, XS_AT + 64 - H))
-        x_codes.append(gather(x_tab[1], offs_t[:], U32, "x_codes1"))
+        wq = [quantise_w(0, XS_AT + 64 - H)]
         d_sc = gather_bytes(ds_tab, user_t[:], "d_sc", XS_AT + 64)
+        x_codes = [gather(x_tab[0], offs_t[:], U32, "x_codes0", "ds_tab")]
+        wq.append(quantise_w(1, "x_tab0"))
+        x_codes.append(gather(x_tab[1], offs_t[:], U32, "x_codes1", "w_grouped1"))
         e_codes = gather(e_tab, shown_t[:], U32, "e_codes", "x_tab1")
         h_codes = tile([P, S], U32, "h_codes", 0)
 

@@ -20,7 +20,8 @@ PACK = 4
 BANK = 512
 E_ROW = 8
 D_ROW = 12
-XS_AT = 4 * W + 512
+XS_AT = 4 * W
+X0_AT = XS_AT + T
 
 
 def tile_picked_ymmr_mmr_p_kernel(
@@ -91,13 +92,14 @@ def tile_picked_ymmr_mmr_p_kernel(
         shown_t = load_list(shown, "shown_t")
         load_scale_rows(es_tab, e_scales, E_ROW)
         load_w(0, 2, PACK)
+        load_w(1, 0, PACK)
         offs_t = load_list(offs, "offs_t")
         for q in (1, 3):
             load_quadrant(nc.sync, xs_tab, x_scales, q)
-        load_w(1, 0, PACK)
+        x_tab = [load_words(x_words[0], "x_tab0", X0_AT)]
         user_t = load_list(user, "user_t")
+        x_tab.append(load_words(x_words[1], "x_tab1"))
         load_scale_rows(ds_tab, d_scales, D_ROW)
-        x_tab = [load_words(x_words[o], "x_tab%d" % o) for o in range(2)]
         e_tab = load_words(e_words[0], "e_tab", 0)
         d_tab = load_words(d_words[0], "d_tab")
 
@@ -113,64 +115,75 @@ def tile_picked_ymmr_mmr_p_kernel(
             return codes, scales
 
         e_sc = gather_bytes(es_tab, shown_t[:], "e_sc")
+        wq = [quantise_w(0, None)]
         x_sc = gather_bytes(xs_tab, offs_t[:], "x_sc")
-        wq = [quantise_w(0, XS_AT + 64 - H)]
-        d_sc = gather_bytes(ds_tab, user_t[:], "d_sc", XS_AT + 64)
-        x_codes = [gather(x_tab[0], offs_t[:], U32, "x_codes0", "ds_tab")]
-        wq.append(quantise_w(1, "x_tab0"))
-        x_codes.append(gather(x_tab[1], offs_t[:], U32, "x_codes1", "w_grouped1"))
+        x_codes = [gather(x_tab[0], offs_t[:], U32, "x_codes0", XS_AT)]
+        wq.append(quantise_w(1, X0_AT))
+        x_codes.append(tile([P, S], U32, "x_codes1", X0_AT + H))
+        for u in range(2):
+            nc.vector.tensor_copy(
+                x_codes[1][:, 256 * u : 256 * (u + 1)], x_tab[1][:].bitcast(U32).indirect(offs_t[:, 16 * u : 16 * (u + 1)])
+            )
+        d_sc = gather_bytes(ds_tab, user_t[:], "d_sc")
         e_codes = gather(e_tab, shown_t[:], U32, "e_codes", "x_tab1")
         h_codes = tile([P, S], U32, "h_codes", 0)
 
         h_grouped = tile([P, S, PACK], BF16, "h_grouped")
         h_scales = tile([P, S], U8, "h_scales")
 
-        def hidden(c):
+        acc = [zpool.tile([P, PACK, P], F32, name="z") for c in range(4)]
+
+        def hidden_pass(c, t, o):
             cols = slice(c * P, (c + 1) * P)
-            acc = zpool.tile([P, PACK, P], F32, name="z")
-            for t in range(PACK):
-                ch = slice(t * P, (t + 1) * P)
-                for o in range(2):
-                    nc.tensor.matmul_mx(
-                        acc[:, t, :],
-                        lhsT=wq[o][0][:, ch].bitcast(FP8X4),
-                        lhsT_scale=wq[o][1][:, ch],
-                        rhs=x_codes[o][:, cols].bitcast(FP8X4),
-                        rhs_scale=x_sc[4 * o : P, cols],
-                        start=(o == 0),
-                        stop=(o == 1),
-                    )
-            nc.scalar.copy(h_grouped[:, cols, :], acc[:].rearrange("p t s -> p s t"))
+            ch = slice(t * P, (t + 1) * P)
+            nc.tensor.matmul_mx(
+                acc[c][:, t, :],
+                lhsT=wq[o][0][:, ch].bitcast(FP8X4),
+                lhsT_scale=wq[o][1][:, ch],
+                rhs=x_codes[o][:, cols].bitcast(FP8X4),
+                rhs_scale=x_sc[4 * o : P, cols],
+                start=(o == 0),
+                stop=(o == 1),
+            )
 
         for c in range(4):
-            hidden(c)
-        for u in range(2):
+            hidden_pass(c, 0, 0)
+        for c in range(4):
+            hidden_pass(c, 0, 1)
+            for t in range(1, PACK):
+                for o in range(2):
+                    hidden_pass(c, t, o)
+            nc.scalar.copy(h_grouped[:, c * P : (c + 1) * P, :], acc[c][:].rearrange("p t s -> p s t"))
+
+        def quantise_h(u):
             cols = slice(u * 2 * P, (u + 1) * 2 * P)
             nc.vector.quantize_mx(
                 h_codes[:, cols].bitcast(FP8X4), h_scales[:, cols], h_grouped[:, cols, :].rearrange("p s t -> p (s t)")
             )
-        hq = [(h_codes[:, c * P : (c + 1) * P], h_scales[:, c * P : (c + 1) * P]) for c in range(4)]
+
+        quantise_h(0)
         d_codes = gather(d_tab, user_t[:], U32, "d_codes", 4 * S)
+        quantise_h(1)
+        hq = [(h_codes[:, c * P : (c + 1) * P], h_scales[:, c * P : (c + 1) * P]) for c in range(4)]
         pair = tile([P, 4, V, 2], F32, "pair")
         near = tile([P, 4, V], F32, "near")
         res = tile([P, 4, V], F32, "res")
         y = [psum.tile([P, 2, V], F32, name="y") for u in range(2)]
 
-        def seen(c):
+        def seen(c, b):
             codes, scales = hq[c]
-            for b in range(2):
-                cols = slice(b * BANK, (b + 1) * BANK)
-                z = zpool.tile([P, BANK], F32, name="z")
-                nc.tensor.matmul_mx(
-                    z[:], lhsT=codes.bitcast(FP8X4), lhsT_scale=scales,
-                    rhs=e_codes[:, cols].bitcast(FP8X4), rhs_scale=e_sc[E_ROW:P, cols], start=True, stop=True,
-                )
-                zd = z[:].rearrange("p (v d) -> p v d", d=D)
-                low = tile([P, P, 2], F32, "low%d_%d" % (c, b))
-                nc.scalar.activation(low[:], zd[:, :, 0:2], COPY, scale=-0.3)
-                nc.vector.scalar_tensor_tensor(
-                    pair[:, c, b * P : (b + 1) * P, :], zd[:, :, 2:4], -0.3, low[:], ALU.mult, ALU.min
-                )
+            cols = slice(b * BANK, (b + 1) * BANK)
+            z = zpool.tile([P, BANK], F32, name="z")
+            nc.tensor.matmul_mx(
+                z[:], lhsT=codes.bitcast(FP8X4), lhsT_scale=scales,
+                rhs=e_codes[:, cols].bitcast(FP8X4), rhs_scale=e_sc[E_ROW:P, cols], start=True, stop=True,
+            )
+            zd = z[:].rearrange("p (v d) -> p v d", d=D)
+            low = tile([P, P, 2], F32, "low%d_%d" % (c, b))
+            nc.scalar.activation(low[:], zd[:, :, 0:2], COPY, scale=-0.3)
+            nc.vector.scalar_tensor_tensor(
+                pair[:, c, b * P : (b + 1) * P, :], zd[:, :, 2:4], -0.3, low[:], ALU.mult, ALU.min
+            )
 
         def intent(c):
             nc.tensor.matmul_mx(
@@ -190,18 +203,28 @@ def tile_picked_ymmr_mmr_p_kernel(
         def store(c0, c1):
             nc.sync.dma_start(out[c0 * P : c1 * P, :].rearrange("(c p) v -> p c v", p=P), res[:, c0:c1, :])
 
-        seen(0)
-        seen(1)
+        def score_on_gpsimd(c0, c1):
+            scaled = tile([P, c1 - c0, V], F32, "scaled%d" % c0)
+            nc.scalar.activation(scaled[:], y[c0 // 2][:, c0 % 2 : c0 % 2 + c1 - c0, :], COPY, scale=0.7)
+            nc.gpsimd.tensor_tensor(res[:, c0:c1, :], scaled[:], near[:, c0:c1, :], ALU.add)
+            store(c0, c1)
+
+        seen(0, 0)
+        seen(0, 1)
+        seen(1, 0)
         intent(0)
-        intent(1)
         nearest(0, 1)
+        score_on_gpsimd(0, 1)
+        seen(1, 1)
+        seen(2, 0)
+        seen(2, 1)
+        intent(1)
         nearest(1, 2)
-        seen(2)
-        score(0, 1)
-        score(1, 2)
-        seen(3)
+        seen(3, 0)
         intent(2)
         intent(3)
+        score(1, 2)
+        seen(3, 1)
         nearest(2, 3)
         nearest(3, 4)
         score(2, 3)

@@ -18,8 +18,7 @@ COPY = mybir.ActivationFunctionType.Copy
 P = 128
 PACK = 4
 BANK = 512
-E_ROW = 8
-D_ROW = 12
+SPREAD = slice(32, 96, 4)
 XS_AT = 4 * W
 X0_AT = XS_AT + T
 
@@ -60,9 +59,12 @@ def tile_picked_ymmr_mmr_p_kernel(
                 src[:, 4 * q : 4 * q + 4, :].bitcast(I32),
             )
 
-        def load_scale_rows(t, src, row):
+        def load_scale_rows(t, src):
+            nc.sync.dma_start(t[SPREAD, :].bitcast(I32), src[0].bitcast(I32))
+
+        def place_scale_rows(plane, picked):
             for r in range(4):
-                nc.sync.dma_start(t[row + r : P : 32, :].bitcast(I32), src[0, r:16:4, :].bitcast(I32))
+                nc.sync.dma_start(plane[r:P:32, :].bitcast(I32), picked[32 + 4 * r : 96 : 16, :].bitcast(I32))
 
         def load_w(o, j0, j1):
             rows = w1[o * 512 : (o + 1) * 512, :].rearrange("(p j) c -> p j c", j=PACK)
@@ -83,6 +85,8 @@ def tile_picked_ymmr_mmr_p_kernel(
         for q in (0, 2):
             load_quadrant(nc.gpsimd, xs_tab, x_scales, q)
         ds_tab = zeroed(nc.vector, G, "ds_tab")
+        e_sc = zeroed(nc.vector, U, "e_sc")
+        d_sc = zeroed(nc.vector, V, "d_sc")
         warm = tile([P, 2], F32, "warm")
         nc.gpsimd.memset(warm[:, 0:1], 0.0)
         nc.scalar.activation(warm[:, 1:2], warm[:, 0:1], COPY)
@@ -90,16 +94,15 @@ def tile_picked_ymmr_mmr_p_kernel(
         w_raw = [tile([P, PACK, H], F32, "w_raw%d" % o) for o in range(2)]
         load_w(0, 0, 2)
         shown_t = load_list(shown, "shown_t")
-        load_scale_rows(es_tab, e_scales, E_ROW)
+        load_scale_rows(es_tab, e_scales)
         load_w(0, 2, PACK)
-        load_w(1, 0, PACK)
+        user_t = load_list(user, "user_t")
+        load_scale_rows(ds_tab, d_scales)
         offs_t = load_list(offs, "offs_t")
+        load_w(1, 0, PACK)
         for q in (1, 3):
             load_quadrant(nc.sync, xs_tab, x_scales, q)
-        x_tab = [load_words(x_words[0], "x_tab0", X0_AT)]
-        user_t = load_list(user, "user_t")
-        x_tab.append(load_words(x_words[1], "x_tab1"))
-        load_scale_rows(ds_tab, d_scales, D_ROW)
+        x_tab = [load_words(x_words[0], "x_tab0", X0_AT), load_words(x_words[1], "x_tab1")]
         e_tab = load_words(e_words[0], "e_tab", 0)
         d_tab = load_words(d_words[0], "d_tab")
 
@@ -114,7 +117,8 @@ def tile_picked_ymmr_mmr_p_kernel(
             nc.vector.quantize_mx(codes[:].bitcast(FP8X4), scales[:], grouped[:])
             return codes, scales
 
-        e_sc = gather_bytes(es_tab, shown_t[:], "e_sc")
+        place_scale_rows(e_sc, gather_bytes(es_tab, shown_t[:], "e_picked"))
+        place_scale_rows(d_sc, gather_bytes(ds_tab, user_t[:], "d_picked"))
         wq = [quantise_w(0, None)]
         x_sc = gather_bytes(xs_tab, offs_t[:], "x_sc")
         x_codes = [gather(x_tab[0], offs_t[:], U32, "x_codes0", XS_AT)]
@@ -124,7 +128,6 @@ def tile_picked_ymmr_mmr_p_kernel(
             nc.vector.tensor_copy(
                 x_codes[1][:, 256 * u : 256 * (u + 1)], x_tab[1][:].bitcast(U32).indirect(offs_t[:, 16 * u : 16 * (u + 1)])
             )
-        d_sc = gather_bytes(ds_tab, user_t[:], "d_sc")
         e_codes = gather(e_tab, shown_t[:], U32, "e_codes", "x_tab1")
         h_codes = tile([P, S], U32, "h_codes", 0)
 
@@ -176,7 +179,7 @@ def tile_picked_ymmr_mmr_p_kernel(
             z = zpool.tile([P, BANK], F32, name="z")
             nc.tensor.matmul_mx(
                 z[:], lhsT=codes.bitcast(FP8X4), lhsT_scale=scales,
-                rhs=e_codes[:, cols].bitcast(FP8X4), rhs_scale=e_sc[E_ROW:P, cols], start=True, stop=True,
+                rhs=e_codes[:, cols].bitcast(FP8X4), rhs_scale=e_sc[:, cols], start=True, stop=True,
             )
             zd = z[:].rearrange("p (v d) -> p v d", d=D)
             low = tile([P, P, 2], F32, "low%d_%d" % (c, b))
@@ -188,7 +191,7 @@ def tile_picked_ymmr_mmr_p_kernel(
         def intent(c):
             nc.tensor.matmul_mx(
                 y[c // 2][:, c % 2, :], lhsT=hq[c][0].bitcast(FP8X4), lhsT_scale=hq[c][1],
-                rhs=d_codes[:].bitcast(FP8X4), rhs_scale=d_sc[D_ROW:P, :], start=True, stop=True,
+                rhs=d_codes[:].bitcast(FP8X4), rhs_scale=d_sc[:], start=True, stop=True,
             )
 
         def nearest(c0, c1):

@@ -18,9 +18,11 @@ COPY = mybir.ActivationFunctionType.Copy
 P = 128
 PACK = 4
 BANK = 512
-SPREAD = slice(32, 96, 4)
-XS_AT = 4 * W
-X0_AT = XS_AT + T
+X1_AT = 0
+XS_AT = 4 * T - 64
+E_AT = XS_AT + T - 64
+ES_AT = E_AT + 4 * W
+X0_AT = ES_AT + 4 * G
 
 
 def tile_picked_ymmr_mmr_p_kernel(
@@ -53,18 +55,14 @@ def tile_picked_ymmr_mmr_p_kernel(
             engine.memset(t[:].bitcast(I32), 0)
             return t
 
-        def load_quadrant(queue, t, src, q):
-            queue.dma_start(
-                t[32 * q : 32 * q + 4 * src.shape[0], :].bitcast(I32),
-                src[:, 4 * q : 4 * q + 4, :].bitcast(I32),
-            )
+        def load_scale_rows(t, first, src):
+            rows = src.rearrange("o q n -> (o q) n")
+            nc.sync.dma_start(t[first : first + 4 * rows.shape[0] : 4, :].bitcast(I32), rows.bitcast(I32))
 
-        def load_scale_rows(t, src):
-            nc.sync.dma_start(t[SPREAD, :].bitcast(I32), src[0].bitcast(I32))
-
-        def place_scale_rows(plane, picked):
+        def place_scale_rows(plane, picked, first):
             for r in range(4):
-                nc.sync.dma_start(plane[r:P:32, :].bitcast(I32), picked[32 + 4 * r : 96 : 16, :].bitcast(I32))
+                src = picked[first + 4 * r : first + 64 : 16, :]
+                nc.sync.dma_start(plane[r:P:32, :].bitcast(I32), src.bitcast(I32))
 
         def load_w(o, j0, j1):
             rows = w1[o * 512 : (o + 1) * 512, :].rearrange("(p j) c -> p j c", j=PACK)
@@ -80,11 +78,10 @@ def tile_picked_ymmr_mmr_p_kernel(
             nc.vector.tensor_copy(t[:], table[:].indirect(offsets))
             return t
 
-        es_tab = zeroed(nc.vector, W, "es_tab")
-        xs_tab = zeroed(nc.gpsimd, T, "xs_tab", XS_AT)
-        for q in (0, 2):
-            load_quadrant(nc.gpsimd, xs_tab, x_scales, q)
-        ds_tab = zeroed(nc.vector, G, "ds_tab")
+        xs_tab = zeroed(nc.vector, T, "xs_tab", XS_AT)
+        es_tab = zeroed(nc.gpsimd, W, "es_tab", ES_AT)
+        ds_tab = zeroed(nc.gpsimd, G, "ds_tab")
+        x_sc = [zeroed(nc.vector, S, "x_sc%d" % o) for o in range(2)]
         e_sc = zeroed(nc.vector, U, "e_sc")
         d_sc = zeroed(nc.vector, V, "d_sc")
         warm = tile([P, 2], F32, "warm")
@@ -93,18 +90,25 @@ def tile_picked_ymmr_mmr_p_kernel(
 
         w_raw = [tile([P, PACK, H], F32, "w_raw%d" % o) for o in range(2)]
         load_w(0, 0, 2)
+        offs_t = load_list(offs, "offs_t")
+        load_scale_rows(xs_tab, 0, x_scales)
         shown_t = load_list(shown, "shown_t")
-        load_scale_rows(es_tab, e_scales)
+        load_scale_rows(es_tab, 32, e_scales)
         load_w(0, 2, PACK)
         user_t = load_list(user, "user_t")
-        load_scale_rows(ds_tab, d_scales)
-        offs_t = load_list(offs, "offs_t")
+        load_scale_rows(ds_tab, 32, d_scales)
         load_w(1, 0, PACK)
-        for q in (1, 3):
-            load_quadrant(nc.sync, xs_tab, x_scales, q)
-        x_tab = [load_words(x_words[0], "x_tab0", X0_AT), load_words(x_words[1], "x_tab1")]
-        e_tab = load_words(e_words[0], "e_tab", 0)
-        d_tab = load_words(d_words[0], "d_tab")
+        x_tab = [load_words(x_words[0], "x_tab0", X0_AT)]
+        x_picked = gather_bytes(xs_tab, offs_t[:], "x_picked")
+        e_picked = gather_bytes(es_tab, shown_t[:], "e_picked")
+        d_picked = gather_bytes(ds_tab, user_t[:], "d_picked")
+        place_scale_rows(x_sc[0], x_picked, 0)
+        x_tab.append(load_words(x_words[1], "x_tab1", X1_AT))
+        place_scale_rows(x_sc[1], x_picked, 64)
+        e_tab = load_words(e_words[0], "e_tab", E_AT)
+        d_tab = load_words(d_words[0], "d_tab", ES_AT)
+        place_scale_rows(e_sc, e_picked, 32)
+        place_scale_rows(d_sc, d_picked, 32)
 
         def quantise_w(o, slot):
             grouped = tile([P, PACK * H], BF16, "w_grouped%d" % o)
@@ -117,19 +121,16 @@ def tile_picked_ymmr_mmr_p_kernel(
             nc.vector.quantize_mx(codes[:].bitcast(FP8X4), scales[:], grouped[:])
             return codes, scales
 
-        place_scale_rows(e_sc, gather_bytes(es_tab, shown_t[:], "e_picked"))
-        place_scale_rows(d_sc, gather_bytes(ds_tab, user_t[:], "d_picked"))
         wq = [quantise_w(0, None)]
-        x_sc = gather_bytes(xs_tab, offs_t[:], "x_sc")
-        x_codes = [gather(x_tab[0], offs_t[:], U32, "x_codes0", XS_AT)]
+        x_codes = [gather(x_tab[0], offs_t[:], U32, "x_codes0")]
         wq.append(quantise_w(1, X0_AT))
         x_codes.append(tile([P, S], U32, "x_codes1", X0_AT + H))
         for u in range(2):
             nc.vector.tensor_copy(
                 x_codes[1][:, 256 * u : 256 * (u + 1)], x_tab[1][:].bitcast(U32).indirect(offs_t[:, 16 * u : 16 * (u + 1)])
             )
-        e_codes = gather(e_tab, shown_t[:], U32, "e_codes", "x_tab1")
-        h_codes = tile([P, S], U32, "h_codes", 0)
+        e_codes = gather(e_tab, shown_t[:], U32, "e_codes", X1_AT)
+        h_codes = tile([P, S], U32, "h_codes", E_AT)
 
         h_grouped = tile([P, S, PACK], BF16, "h_grouped")
         h_scales = tile([P, S], U8, "h_scales")
@@ -144,7 +145,7 @@ def tile_picked_ymmr_mmr_p_kernel(
                 lhsT=wq[o][0][:, ch].bitcast(FP8X4),
                 lhsT_scale=wq[o][1][:, ch],
                 rhs=x_codes[o][:, cols].bitcast(FP8X4),
-                rhs_scale=x_sc[4 * o : P, cols],
+                rhs_scale=x_sc[o][:, cols],
                 start=(o == 0),
                 stop=(o == 1),
             )
@@ -165,7 +166,7 @@ def tile_picked_ymmr_mmr_p_kernel(
             )
 
         quantise_h(0)
-        d_codes = gather(d_tab, user_t[:], U32, "d_codes", 4 * S)
+        d_codes = gather(d_tab, user_t[:], U32, "d_codes", E_AT + 4 * S)
         quantise_h(1)
         hq = [(h_codes[:, c * P : (c + 1) * P], h_scales[:, c * P : (c + 1) * P]) for c in range(4)]
         pair = tile([P, 4, V, 2], F32, "pair")

@@ -23,6 +23,7 @@ XS_AT = 4 * T - 64
 E_AT = XS_AT + T - 64
 ES_AT = E_AT + 4 * W
 X0_AT = ES_AT + 4 * G
+H_AT = X0_AT + 4 * T
 
 
 def tile_picked_ymmr_mmr_p_kernel(
@@ -100,14 +101,14 @@ def tile_picked_ymmr_mmr_p_kernel(
         load_w(1, 0, PACK)
         x_tab = [load_words(x_words[0], "x_tab0", X0_AT)]
         x_picked = gather_bytes(xs_tab, offs_t[:], "x_picked")
-        e_picked = gather_bytes(es_tab, shown_t[:], "e_picked")
+        e_picked = gather_bytes(es_tab, shown_t[:], "e_picked", H_AT)
         d_picked = gather_bytes(ds_tab, user_t[:], "d_picked")
         place_scale_rows(x_sc[0], x_picked, 0)
         x_tab.append(load_words(x_words[1], "x_tab1", X1_AT))
         place_scale_rows(x_sc[1], x_picked, 64)
         e_tab = load_words(e_words[0], "e_tab", E_AT)
-        d_tab = load_words(d_words[0], "d_tab", ES_AT)
         place_scale_rows(e_sc, e_picked, 32)
+        d_tab = load_words(d_words[0], "d_tab", ES_AT)
         place_scale_rows(d_sc, d_picked, 32)
 
         def quantise_w(o, slot):
@@ -130,7 +131,7 @@ def tile_picked_ymmr_mmr_p_kernel(
                 x_codes[1][:, 256 * u : 256 * (u + 1)], x_tab[1][:].bitcast(U32).indirect(offs_t[:, 16 * u : 16 * (u + 1)])
             )
         e_codes = gather(e_tab, shown_t[:], U32, "e_codes", X1_AT)
-        h_codes = tile([P, S], U32, "h_codes", E_AT)
+        h_codes = tile([P, S], U32, "h_codes", H_AT)
 
         h_grouped = tile([P, S, PACK], BF16, "h_grouped")
         h_scales = tile([P, S], U8, "h_scales")
@@ -202,16 +203,16 @@ def tile_picked_ymmr_mmr_p_kernel(
             nc.vector.scalar_tensor_tensor(
                 res[:, c0:c1, :], y[c0 // 2][:, c0 % 2 : c0 % 2 + c1 - c0, :], 0.7, near[:, c0:c1, :], ALU.mult, ALU.add
             )
-            store(c0, c1)
+            store(nc.sync, c0, c1)
 
-        def store(c0, c1):
-            nc.sync.dma_start(out[c0 * P : c1 * P, :].rearrange("(c p) v -> p c v", p=P), res[:, c0:c1, :])
+        def store(queue, c0, c1):
+            queue.dma_start(out[c0 * P : c1 * P, :].rearrange("(c p) v -> p c v", p=P), res[:, c0:c1, :])
 
         def score_on_gpsimd(c0, c1):
             scaled = tile([P, c1 - c0, V], F32, "scaled%d" % c0)
             nc.scalar.activation(scaled[:], y[c0 // 2][:, c0 % 2 : c0 % 2 + c1 - c0, :], COPY, scale=0.7)
             nc.gpsimd.tensor_tensor(res[:, c0:c1, :], scaled[:], near[:, c0:c1, :], ALU.add)
-            store(c0, c1)
+            store(nc.scalar, c0, c1)
 
         seen(0, 0)
         seen(0, 1)

@@ -111,20 +111,21 @@ def tile_picked_ymmr_mmr_p_kernel(
         d_tab = load_words(d_words[0], "d_tab", ES_AT)
         place_scale_rows(d_sc, d_picked, 32)
 
-        def quantise_w(o, slot):
+        def quantise_w(o, slot, on_scalar):
             grouped = tile([P, PACK * H], BF16, "w_grouped%d" % o)
-            nc.scalar.copy(
-                grouped[:].rearrange("p (t m j) -> p m t j", t=4, j=PACK),
-                w_raw[o][:].rearrange("p j (m t) -> p m t j", t=4),
-            )
+            dst = grouped[:].rearrange("p (t m j) -> p m t j", t=4, j=PACK)
+            src = w_raw[o][:].rearrange("p j (m t) -> p m t j", t=4)
+            nc.scalar.copy(dst[:, :, 0:on_scalar, :], src[:, :, 0:on_scalar, :])
+            if on_scalar < PACK:
+                nc.vector.tensor_copy(dst[:, :, on_scalar:PACK, :], src[:, :, on_scalar:PACK, :])
             codes = tile([P, H], U32, "w_codes%d" % o)
             scales = tile([P, H], U8, "w_scales%d" % o, slot)
             nc.vector.quantize_mx(codes[:].bitcast(FP8X4), scales[:], grouped[:])
             return codes, scales
 
-        wq = [quantise_w(0, None)]
+        wq = [quantise_w(0, None, PACK)]
         x_codes = [gather(x_tab[0], offs_t[:], U32, "x_codes0")]
-        wq.append(quantise_w(1, X0_AT))
+        wq.append(quantise_w(1, X0_AT, 2))
         x_codes.append(tile([P, S], U32, "x_codes1", X0_AT + H))
         for u in range(2):
             nc.vector.tensor_copy(

@@ -24,6 +24,8 @@ E_AT = XS_AT + T - 64
 ES_AT = E_AT + 4 * W
 X0_AT = ES_AT + 4 * G
 H_AT = X0_AT + 4 * T
+PICKED_AT = H_AT + 4 * S - 64
+E1_AT = PICKED_AT + U - 64
 
 
 def tile_picked_ymmr_mmr_p_kernel(
@@ -101,7 +103,7 @@ def tile_picked_ymmr_mmr_p_kernel(
         load_w(1, 0, PACK)
         x_tab = [load_words(x_words[0], "x_tab0", X0_AT)]
         x_picked = gather_bytes(xs_tab, offs_t[:], "x_picked")
-        e_picked = gather_bytes(es_tab, shown_t[:], "e_picked", H_AT)
+        e_picked = gather_bytes(es_tab, shown_t[:], "e_picked", PICKED_AT)
         d_picked = gather_bytes(ds_tab, user_t[:], "d_picked")
         place_scale_rows(x_sc[0], x_picked, 0)
         x_tab.append(load_words(x_words[1], "x_tab1", X1_AT))
@@ -111,27 +113,26 @@ def tile_picked_ymmr_mmr_p_kernel(
         d_tab = load_words(d_words[0], "d_tab", ES_AT)
         place_scale_rows(d_sc, d_picked, 32)
 
-        def quantise_w(o, slot, on_scalar):
+        def quantise_w(o, slot):
             grouped = tile([P, PACK * H], BF16, "w_grouped%d" % o)
-            dst = grouped[:].rearrange("p (t m j) -> p m t j", t=4, j=PACK)
-            src = w_raw[o][:].rearrange("p j (m t) -> p m t j", t=4)
-            nc.scalar.copy(dst[:, :, 0:on_scalar, :], src[:, :, 0:on_scalar, :])
-            if on_scalar < PACK:
-                nc.vector.tensor_copy(dst[:, :, on_scalar:PACK, :], src[:, :, on_scalar:PACK, :])
+            nc.scalar.copy(
+                grouped[:].rearrange("p (t m j) -> p m t j", t=4, j=PACK),
+                w_raw[o][:].rearrange("p j (m t) -> p m t j", t=4),
+            )
             codes = tile([P, H], U32, "w_codes%d" % o)
             scales = tile([P, H], U8, "w_scales%d" % o, slot)
             nc.vector.quantize_mx(codes[:].bitcast(FP8X4), scales[:], grouped[:])
             return codes, scales
 
-        wq = [quantise_w(0, None, PACK)]
+        wq = [quantise_w(0, None)]
         x_codes = [gather(x_tab[0], offs_t[:], U32, "x_codes0")]
-        wq.append(quantise_w(1, X0_AT, 2))
+        wq.append(quantise_w(1, X0_AT))
         x_codes.append(tile([P, S], U32, "x_codes1", X0_AT + H))
         for u in range(2):
             nc.vector.tensor_copy(
                 x_codes[1][:, 256 * u : 256 * (u + 1)], x_tab[1][:].bitcast(U32).indirect(offs_t[:, 16 * u : 16 * (u + 1)])
             )
-        e_codes = gather(e_tab, shown_t[:], U32, "e_codes", X1_AT)
+        e_codes = [gather(e_tab, shown_t[:, 0:32], U32, "e_codes0", X1_AT)]
         h_codes = tile([P, S], U32, "h_codes", H_AT)
 
         h_grouped = tile([P, S, PACK], BF16, "h_grouped")
@@ -152,8 +153,18 @@ def tile_picked_ymmr_mmr_p_kernel(
                 stop=(o == 1),
             )
 
+        def warm_up(codes, scales):
+            for r in range(2):
+                idle = psum.tile([P, BANK], F32, name="y")
+                nc.tensor.matmul_mx(
+                    idle[:], lhsT=wq[0][0][:, 0:P].bitcast(FP8X4), lhsT_scale=wq[0][1][:, 0:P],
+                    rhs=codes[:].bitcast(FP8X4), rhs_scale=scales[:], start=True, stop=True,
+                )
+
+        warm_up(*wq[0])
         for c in range(4):
             hidden_pass(c, 0, 0)
+        warm_up(x_codes[0], x_sc[0])
         for c in range(4):
             hidden_pass(c, 0, 1)
             for t in range(1, PACK):
@@ -168,8 +179,9 @@ def tile_picked_ymmr_mmr_p_kernel(
             )
 
         quantise_h(0)
-        d_codes = gather(d_tab, user_t[:], U32, "d_codes", E_AT + 4 * S)
+        e_codes.append(gather(e_tab, shown_t[:, 32:64], U32, "e_codes1", E1_AT))
         quantise_h(1)
+        d_codes = gather(d_tab, user_t[:], U32, "d_codes", E_AT)
         hq = [(h_codes[:, c * P : (c + 1) * P], h_scales[:, c * P : (c + 1) * P]) for c in range(4)]
         pair = tile([P, 4, V, 2], F32, "pair")
         near = tile([P, 4, V], F32, "near")
@@ -182,7 +194,7 @@ def tile_picked_ymmr_mmr_p_kernel(
             z = zpool.tile([P, BANK], F32, name="z")
             nc.tensor.matmul_mx(
                 z[:], lhsT=codes.bitcast(FP8X4), lhsT_scale=scales,
-                rhs=e_codes[:, cols].bitcast(FP8X4), rhs_scale=e_sc[:, cols], start=True, stop=True,
+                rhs=e_codes[b][:].bitcast(FP8X4), rhs_scale=e_sc[:, cols], start=True, stop=True,
             )
             zd = z[:].rearrange("p (v d) -> p v d", d=D)
             low = tile([P, P, 2], F32, "low%d_%d" % (c, b))
@@ -204,33 +216,24 @@ def tile_picked_ymmr_mmr_p_kernel(
             nc.vector.scalar_tensor_tensor(
                 res[:, c0:c1, :], y[c0 // 2][:, c0 % 2 : c0 % 2 + c1 - c0, :], 0.7, near[:, c0:c1, :], ALU.mult, ALU.add
             )
-            store(nc.sync, c0, c1)
+            store(c0, c1)
 
-        def store(queue, c0, c1):
-            queue.dma_start(out[c0 * P : c1 * P, :].rearrange("(c p) v -> p c v", p=P), res[:, c0:c1, :])
+        def store(c0, c1):
+            nc.sync.dma_start(out[c0 * P : c1 * P, :].rearrange("(c p) v -> p c v", p=P), res[:, c0:c1, :])
 
-        def score_on_gpsimd(c0, c1):
-            scaled = tile([P, c1 - c0, V], F32, "scaled%d" % c0)
-            nc.scalar.activation(scaled[:], y[c0 // 2][:, c0 % 2 : c0 % 2 + c1 - c0, :], COPY, scale=0.7)
-            nc.gpsimd.tensor_tensor(res[:, c0:c1, :], scaled[:], near[:, c0:c1, :], ALU.add)
-            store(nc.scalar, c0, c1)
-
-        seen(0, 0)
-        seen(0, 1)
-        seen(1, 0)
-        intent(0)
-        nearest(0, 1)
-        score_on_gpsimd(0, 1)
-        seen(1, 1)
+        for b in range(2):
+            seen(0, b)
+            seen(1, b)
         seen(2, 0)
+        nearest(0, 2)
         seen(2, 1)
+        intent(0)
         intent(1)
-        nearest(1, 2)
         seen(3, 0)
+        score(0, 2)
+        seen(3, 1)
         intent(2)
         intent(3)
-        score(1, 2)
-        seen(3, 1)
         nearest(2, 3)
         nearest(3, 4)
         score(2, 3)

@@ -18,12 +18,15 @@ COPY = mybir.ActivationFunctionType.Copy
 P = 128
 PACK = 4
 BANK = 512
-X1_AT = 0
-XS_AT = 4 * T - 64
-E_AT = XS_AT + T - 64
-ES_AT = E_AT + 4 * W
-X0_AT = ES_AT + 4 * G
-H_AT = X0_AT + 4 * T
+Z_BANKS = ((0, 1), (2, 3), (4, 0), (6, 2))
+XS_AT = 0
+X0_AT = XS_AT + T - 64
+DS_AT = X0_AT + 4 * T
+X1_AT = DS_AT + G - 64
+D_AT = X1_AT + 4 * T
+ES_AT = D_AT + 4 * G - 64
+E_AT = ES_AT + W - 64
+H_AT = E_AT + 4 * W
 PICKED_AT = H_AT + 4 * S - 64
 E1_AT = PICKED_AT + U - 64
 
@@ -35,8 +38,10 @@ def tile_picked_ymmr_mmr_p_kernel(
     with ExitStack() as ctx:
         keep = ctx.enter_context(tc.tile_pool(name="keep", bufs=1))
         reuse = ctx.enter_context(tc.tile_pool(name="reuse", bufs=1))
-        psum = ctx.enter_context(tc.psum_pool(name="psum", bufs=2))
-        zpool = ctx.enter_context(tc.psum_pool(name="zpool", bufs=6))
+        psum = ctx.enter_context(tc.psum_pool(name="psum", bufs=1))
+
+        def bank(shape, name, number):
+            return psum.tile(shape, F32, name=name, tag="bank%d" % number)
 
         def tile(shape, dtype, name, slot=None):
             if isinstance(slot, int):
@@ -62,9 +67,9 @@ def tile_picked_ymmr_mmr_p_kernel(
             rows = src.rearrange("o q n -> (o q) n")
             nc.sync.dma_start(t[first : first + 4 * rows.shape[0] : 4, :].bitcast(I32), rows.bitcast(I32))
 
-        def place_scale_rows(plane, picked, first):
+        def place_scale_rows(plane, picked, first, step, width):
             for r in range(4):
-                src = picked[first + 4 * r : first + 64 : 16, :]
+                src = picked[first + step * r : first + 16 * step : 4 * step, 0:width]
                 nc.sync.dma_start(plane[r:P:32, :].bitcast(I32), src.bitcast(I32))
 
         def load_w(o, j0, j1):
@@ -81,37 +86,39 @@ def tile_picked_ymmr_mmr_p_kernel(
             nc.vector.tensor_copy(t[:], table[:].indirect(offsets))
             return t
 
-        xs_tab = zeroed(nc.vector, T, "xs_tab", XS_AT)
+        xs_tab = tile([P, T], U8, "xs_tab", XS_AT)
+        nc.vector.memset(xs_tab[0:96, :].bitcast(I32), 0)
         es_tab = zeroed(nc.gpsimd, W, "es_tab", ES_AT)
-        ds_tab = zeroed(nc.gpsimd, G, "ds_tab")
-        x_sc = [zeroed(nc.vector, S, "x_sc%d" % o) for o in range(2)]
+        ds_tab = zeroed(nc.gpsimd, G, "ds_tab", DS_AT)
+        x0_sc = zeroed(nc.vector, S, "x0_sc")
+        xd_sc = zeroed(nc.vector, S + V, "xd_sc")
+        x_sc = [x0_sc[:], xd_sc[:, 0:S]]
+        d_sc = xd_sc[:, S : S + V]
         e_sc = zeroed(nc.vector, U, "e_sc")
-        d_sc = zeroed(nc.vector, V, "d_sc")
-        warm = tile([P, 2], F32, "warm")
-        nc.gpsimd.memset(warm[:, 0:1], 0.0)
-        nc.scalar.activation(warm[:, 1:2], warm[:, 0:1], COPY)
 
         w_raw = [tile([P, PACK, H], F32, "w_raw%d" % o) for o in range(2)]
-        load_w(0, 0, 2)
         offs_t = load_list(offs, "offs_t")
-        load_scale_rows(xs_tab, 0, x_scales)
+        nc.sync.dma_start(xs_tab[96:P, :].bitcast(I32), x_scales.rearrange("o q n -> (o q) n").bitcast(I32))
+        load_w(0, 0, PACK)
+        user_t = load_list(user, "user_t")
+        nc.sync.dma_start(ds_tab[112:P, :].bitcast(I32), d_scales[0].bitcast(I32))
         shown_t = load_list(shown, "shown_t")
         load_scale_rows(es_tab, 32, e_scales)
-        load_w(0, 2, PACK)
-        user_t = load_list(user, "user_t")
-        load_scale_rows(ds_tab, 32, d_scales)
         load_w(1, 0, PACK)
+        xd_picked = tile([P, S + V], U8, "xd_picked")
+        nc.vector.tensor_copy(xd_picked[:, 0:S], xs_tab[:].indirect(offs_t[:]))
+        nc.vector.tensor_copy(xd_picked[:, S : S + V], ds_tab[:].indirect(user_t[:]))
+        e_picked = tile([P, U], U8, "e_picked", PICKED_AT)
+        nc.vector.tensor_copy(
+            e_picked[:].rearrange("p (u d v) -> p u v d", u=2, d=D), es_tab[:].indirect(shown_t[:])
+        )
+        place_scale_rows(x0_sc, xd_picked, 96, 1, S)
         x_tab = [load_words(x_words[0], "x_tab0", X0_AT)]
-        x_picked = gather_bytes(xs_tab, offs_t[:], "x_picked")
-        e_picked = gather_bytes(es_tab, shown_t[:], "e_picked", PICKED_AT)
-        d_picked = gather_bytes(ds_tab, user_t[:], "d_picked")
-        place_scale_rows(x_sc[0], x_picked, 0)
+        place_scale_rows(xd_sc, xd_picked, 112, 1, S + V)
         x_tab.append(load_words(x_words[1], "x_tab1", X1_AT))
-        place_scale_rows(x_sc[1], x_picked, 64)
         e_tab = load_words(e_words[0], "e_tab", E_AT)
-        place_scale_rows(e_sc, e_picked, 32)
-        d_tab = load_words(d_words[0], "d_tab", ES_AT)
-        place_scale_rows(d_sc, d_picked, 32)
+        place_scale_rows(e_sc, e_picked, 32, 4, U)
+        d_tab = load_words(d_words[0], "d_tab", D_AT)
 
         def quantise_w(o, slot):
             grouped = tile([P, PACK * H], BF16, "w_grouped%d" % o)
@@ -124,117 +131,151 @@ def tile_picked_ymmr_mmr_p_kernel(
             nc.vector.quantize_mx(codes[:].bitcast(FP8X4), scales[:], grouped[:])
             return codes, scales
 
-        wq = [quantise_w(0, None)]
-        x_codes = [gather(x_tab[0], offs_t[:], U32, "x_codes0")]
-        wq.append(quantise_w(1, X0_AT))
-        x_codes.append(tile([P, S], U32, "x_codes1", X0_AT + H))
-        for u in range(2):
+        def gather_pieces(t, table, edges):
+            for a, b in zip(edges, edges[1:]):
+                nc.vector.tensor_copy(t[:, a:b], table[:].bitcast(U32).indirect(offs_t[:, a // 16 : b // 16]))
+
+        def gather_seen(u, slot):
+            t = tile([P, D, P], U32, "e_codes%d" % u, slot)
             nc.vector.tensor_copy(
-                x_codes[1][:, 256 * u : 256 * (u + 1)], x_tab[1][:].bitcast(U32).indirect(offs_t[:, 16 * u : 16 * (u + 1)])
+                t[:].rearrange("p d v -> p v d"), e_tab[:].bitcast(U32).indirect(shown_t[:, 32 * u : 32 * (u + 1)])
             )
-        e_codes = [gather(e_tab, shown_t[:, 0:32], U32, "e_codes0", X1_AT)]
-        h_codes = tile([P, S], U32, "h_codes", H_AT)
+            return t
 
-        h_grouped = tile([P, S, PACK], BF16, "h_grouped")
-        h_scales = tile([P, S], U8, "h_scales")
+        wq = [quantise_w(0, None)]
+        x_codes = [tile([P, S], U32, "x_codes0")]
+        gather_pieces(x_codes[0], x_tab[0], (0, 256, 512))
+        wq.append(quantise_w(1, X0_AT + 64))
+        x_codes.append(tile([P, S], U32, "x_codes1", X0_AT + 64 + H))
+        gather_pieces(x_codes[1], x_tab[1], (0, 128, 256, 512))
 
-        acc = [zpool.tile([P, PACK, P], F32, name="z") for c in range(4)]
+        h_grouped = [tile([P, 2 * P, PACK], BF16, "h_grouped%d" % u) for u in range(2)]
+        acc = [bank([P, PACK, P], "acc%d" % c, 6 + c % 2) for c in range(4)]
 
-        def hidden_pass(c, t, o):
+        def hidden_pass(c, o):
             cols = slice(c * P, (c + 1) * P)
-            ch = slice(t * P, (t + 1) * P)
-            nc.tensor.matmul_mx(
-                acc[c][:, t, :],
-                lhsT=wq[o][0][:, ch].bitcast(FP8X4),
-                lhsT_scale=wq[o][1][:, ch],
-                rhs=x_codes[o][:, cols].bitcast(FP8X4),
-                rhs_scale=x_sc[o][:, cols],
-                start=(o == 0),
-                stop=(o == 1),
-            )
-
-        def warm_up(codes, scales):
-            for r in range(2):
-                idle = psum.tile([P, BANK], F32, name="y")
+            for t in range(PACK):
+                ch = slice(t * P, (t + 1) * P)
                 nc.tensor.matmul_mx(
-                    idle[:], lhsT=wq[0][0][:, 0:P].bitcast(FP8X4), lhsT_scale=wq[0][1][:, 0:P],
-                    rhs=codes[:].bitcast(FP8X4), rhs_scale=scales[:], start=True, stop=True,
+                    acc[c][:, t, :],
+                    lhsT=wq[o][0][:, ch].bitcast(FP8X4),
+                    lhsT_scale=wq[o][1][:, ch],
+                    rhs=x_codes[o][:, cols].bitcast(FP8X4),
+                    rhs_scale=x_sc[o][:, cols],
+                    start=(o == 0 and t == 0),
+                    stop=(o == 1 and t == PACK - 1),
                 )
 
-        warm_up(*wq[0])
+        for c in range(2):
+            hidden_pass(c, 0)
         for c in range(4):
-            hidden_pass(c, 0, 0)
-        warm_up(x_codes[0], x_sc[0])
-        for c in range(4):
-            hidden_pass(c, 0, 1)
-            for t in range(1, PACK):
-                for o in range(2):
-                    hidden_pass(c, t, o)
-            nc.scalar.copy(h_grouped[:, c * P : (c + 1) * P, :], acc[c][:].rearrange("p t s -> p s t"))
+            if c >= 2:
+                hidden_pass(c, 0)
+            hidden_pass(c, 1)
+            nc.scalar.copy(h_grouped[c // 2][:, c % 2 * P : (c % 2 + 1) * P, :], acc[c][:].rearrange("p t s -> p s t"))
+
+        h_codes = tile([P, S], U32, "h_codes", H_AT)
+        h_scales = tile([P, S], U8, "h_scales")
+        hq = [(h_codes[:, c * P : (c + 1) * P], h_scales[:, c * P : (c + 1) * P]) for c in range(4)]
 
         def quantise_h(u):
             cols = slice(u * 2 * P, (u + 1) * 2 * P)
             nc.vector.quantize_mx(
-                h_codes[:, cols].bitcast(FP8X4), h_scales[:, cols], h_grouped[:, cols, :].rearrange("p s t -> p (s t)")
+                h_codes[:, cols].bitcast(FP8X4), h_scales[:, cols], h_grouped[u][:].rearrange("p s t -> p (s t)")
             )
 
+        e_codes = [gather_seen(0, X1_AT)]
         quantise_h(0)
-        e_codes.append(gather(e_tab, shown_t[:, 32:64], U32, "e_codes1", E1_AT))
+        e_codes.append(gather_seen(1, E1_AT))
         quantise_h(1)
-        d_codes = gather(d_tab, user_t[:], U32, "d_codes", E_AT)
-        hq = [(h_codes[:, c * P : (c + 1) * P], h_scales[:, c * P : (c + 1) * P]) for c in range(4)]
-        pair = tile([P, 4, V, 2], F32, "pair")
-        near = tile([P, 4, V], F32, "near")
         res = tile([P, 4, V], F32, "res")
-        y = [psum.tile([P, 2, V], F32, name="y") for u in range(2)]
+        z = [[bank([P, 2, 2, P], "z%d_%d" % (c, b), Z_BANKS[c][b]) for b in range(2)] for c in range(4)]
+        low = [[tile([P, 2, P], F32, "low%d_%d" % (c, i)) for i in range(D)] for c in range(4)]
 
-        def seen(c, b):
-            codes, scales = hq[c]
-            cols = slice(b * BANK, (b + 1) * BANK)
-            z = zpool.tile([P, BANK], F32, name="z")
+        def seen(c, u, b):
+            group, half = (u, c) if c < 2 else (c, u)
+            first = u * BANK + b * V
             nc.tensor.matmul_mx(
-                z[:], lhsT=codes.bitcast(FP8X4), lhsT_scale=scales,
-                rhs=e_codes[b][:].bitcast(FP8X4), rhs_scale=e_sc[:, cols], start=True, stop=True,
+                z[group][b][:, half, :, :].rearrange("p d v -> p (d v)"), lhsT=hq[c][0].bitcast(FP8X4), lhsT_scale=hq[c][1],
+                rhs=e_codes[u][:, 2 * b : 2 * b + 2, :].rearrange("p d v -> p (d v)").bitcast(FP8X4),
+                rhs_scale=e_sc[:, first : first + V], start=True, stop=True,
             )
-            zd = z[:].rearrange("p (v d) -> p v d", d=D)
-            low = tile([P, P, 2], F32, "low%d_%d" % (c, b))
-            nc.scalar.activation(low[:], zd[:, :, 0:2], COPY, scale=-0.3)
+
+        def scaled(group, i, out):
+            nc.scalar.activation(out[:], z[group][i // 2][:, :, i % 2, :], COPY, scale=-0.3)
+
+        def lower(group, i, out, prior, half=slice(0, 2)):
             nc.vector.scalar_tensor_tensor(
-                pair[:, c, b * P : (b + 1) * P, :], zd[:, :, 2:4], -0.3, low[:], ALU.mult, ALU.min
+                out[:, half, :], z[group][i // 2][:, half, i % 2, :], -0.3, prior[:, half, :], ALU.mult, ALU.min
             )
 
-        def intent(c):
-            nc.tensor.matmul_mx(
-                y[c // 2][:, c % 2, :], lhsT=hq[c][0].bitcast(FP8X4), lhsT_scale=hq[c][1],
-                rhs=d_codes[:].bitcast(FP8X4), rhs_scale=d_sc[:], start=True, stop=True,
-            )
+        def next_seen(group, i, half=slice(0, 2)):
+            lower(group, i, low[group][i], low[group][i - 1], half)
 
-        def nearest(c0, c1):
-            nc.vector.tensor_tensor(near[:, c0:c1, :], pair[:, c0:c1, :, 0], pair[:, c0:c1, :, 1], ALU.min)
+        def intent(pair):
+            y = bank([P, 2, V], "y%d" % pair, 5 + 2 * pair)
+            for i in range(2):
+                codes, scales = hq[2 * pair + i]
+                nc.tensor.matmul_mx(
+                    y[:, i, :], lhsT=codes.bitcast(FP8X4), lhsT_scale=scales,
+                    rhs=d_codes[:].bitcast(FP8X4), rhs_scale=d_sc, start=True, stop=True,
+                )
+            return y
 
-        def score(c0, c1):
-            nc.vector.scalar_tensor_tensor(
-                res[:, c0:c1, :], y[c0 // 2][:, c0 % 2 : c0 % 2 + c1 - c0, :], 0.7, near[:, c0:c1, :], ALU.mult, ALU.add
-            )
-            store(c0, c1)
+        def nearest(c):
+            return low[c][D - 1][:].rearrange("p u v -> p (u v)")
 
         def store(c0, c1):
             nc.sync.dma_start(out[c0 * P : c1 * P, :].rearrange("(c p) v -> p c v", p=P), res[:, c0:c1, :])
 
-        for b in range(2):
-            seen(0, b)
-            seen(1, b)
-        seen(2, 0)
-        nearest(0, 2)
-        seen(2, 1)
-        intent(0)
-        intent(1)
-        seen(3, 0)
-        score(0, 2)
-        seen(3, 1)
-        intent(2)
-        intent(3)
-        nearest(2, 3)
-        nearest(3, 4)
-        score(2, 3)
-        score(3, 4)
+        def add_scaled(u):
+            users = slice(u * P, (u + 1) * P)
+            nc.gpsimd.tensor_tensor(res[:, 0:2, users], y_scaled[u][:], low[u][D - 1][:], ALU.add)
+
+        def score(c, users):
+            nc.vector.scalar_tensor_tensor(res[:, c, users], y[1][:, c - 2, users], 0.7, nearest(c)[:, users], ALU.mult, ALU.add)
+
+        for u in range(2):
+            for b in range(2):
+                seen(0, u, b)
+                seen(1, u, b)
+        d_codes = gather(d_tab, user_t[:], U32, "d_codes", E_AT)
+        third = tile([P, 2, P], F32, "third")
+        scaled(0, 0, low[0][0])
+        scaled(0, 2, third)
+        scaled(1, 0, low[1][0])
+        seen(2, 0, 0)
+        seen(2, 1, 0)
+        scaled(2, 0, low[2][0])
+        y = [intent(0)]
+        y_scaled = [tile([P, 2, P], F32, "y_scaled%d" % u) for u in range(2)]
+        nc.scalar.activation(y_scaled[0][:], y[0][:, :, 0:P], COPY, scale=0.7)
+        seen(3, 0, 0)
+        seen(3, 1, 0)
+        scaled(3, 0, low[3][0])
+        nc.scalar.activation(y_scaled[1][:], y[0][:, :, P:V], COPY, scale=0.7)
+        next_seen(0, 1)
+        lower(0, 3, low[0][2], third)
+        next_seen(1, 1)
+        for c in range(2, 4):
+            seen(c, 0, 1)
+            seen(c, 1, 1)
+        y.append(intent(1))
+        nc.vector.tensor_tensor(low[0][3][:], low[0][1][:], low[0][2][:], ALU.min)
+        add_scaled(0)
+        next_seen(1, 2)
+        next_seen(2, 1)
+        next_seen(1, 3)
+        add_scaled(1)
+        store(0, 2)
+        next_seen(2, 2)
+        next_seen(3, 1)
+        next_seen(2, 3)
+        next_seen(3, 2)
+        score(2, slice(0, V))
+        store(2, 3)
+        for u in range(2):
+            next_seen(3, 3, slice(u, u + 1))
+        for u in range(2):
+            score(3, slice(u * P, (u + 1) * P))
+        store(3, 4)

@@ -27,7 +27,7 @@ D_AT = X1_AT + 4 * T
 ES_AT = D_AT + 4 * G - 64
 E_AT = ES_AT + W - 64
 H_AT = E_AT + 4 * W
-PICKED_AT = H_AT + 4 * S - 64
+PICKED_AT = H_AT + 4 * (S - P) - 64
 E1_AT = PICKED_AT + U - 64
 
 
@@ -67,10 +67,10 @@ def tile_picked_ymmr_mmr_p_kernel(
             rows = src.rearrange("o q n -> (o q) n")
             nc.sync.dma_start(t[first : first + 4 * rows.shape[0] : 4, :].bitcast(I32), rows.bitcast(I32))
 
-        def place_scale_rows(plane, picked, first, step, width):
+        def place_scale_rows(plane, row, picked, first, step, width):
             for r in range(4):
                 src = picked[first + step * r : first + 16 * step : 4 * step, 0:width]
-                nc.sync.dma_start(plane[r:P:32, :].bitcast(I32), src.bitcast(I32))
+                nc.sync.dma_start(plane[row + r : P : 32, :].bitcast(I32), src.bitcast(I32))
 
         def load_w(o, j0, j1):
             rows = w1[o * 512 : (o + 1) * 512, :].rearrange("(p j) c -> p j c", j=PACK)
@@ -92,8 +92,8 @@ def tile_picked_ymmr_mmr_p_kernel(
         ds_tab = zeroed(nc.gpsimd, G, "ds_tab", DS_AT)
         x0_sc = zeroed(nc.vector, S, "x0_sc")
         xd_sc = zeroed(nc.vector, S + V, "xd_sc")
-        x_sc = [x0_sc[:], xd_sc[:, 0:S]]
-        d_sc = xd_sc[:, S : S + V]
+        x_sc = [x0_sc[:], xd_sc[4:P, 0:S]]
+        d_sc = xd_sc[4:P, S : S + V]
         e_sc = zeroed(nc.vector, U, "e_sc")
 
         w_raw = [tile([P, PACK, H], F32, "w_raw%d" % o) for o in range(2)]
@@ -103,7 +103,7 @@ def tile_picked_ymmr_mmr_p_kernel(
         user_t = load_list(user, "user_t")
         nc.sync.dma_start(ds_tab[112:P, :].bitcast(I32), d_scales[0].bitcast(I32))
         shown_t = load_list(shown, "shown_t")
-        load_scale_rows(es_tab, 32, e_scales)
+        load_scale_rows(es_tab, 0, e_scales)
         load_w(1, 0, PACK)
         xd_picked = tile([P, S + V], U8, "xd_picked")
         nc.vector.tensor_copy(xd_picked[:, 0:S], xs_tab[:].indirect(offs_t[:]))
@@ -112,12 +112,12 @@ def tile_picked_ymmr_mmr_p_kernel(
         nc.vector.tensor_copy(
             e_picked[:].rearrange("p (u d v) -> p u v d", u=2, d=D), es_tab[:].indirect(shown_t[:])
         )
-        place_scale_rows(x0_sc, xd_picked, 96, 1, S)
+        place_scale_rows(x0_sc, 0, xd_picked, 96, 1, S)
         x_tab = [load_words(x_words[0], "x_tab0", X0_AT)]
-        place_scale_rows(xd_sc, xd_picked, 112, 1, S + V)
+        place_scale_rows(xd_sc, 4, xd_picked, 112, 1, S + V)
         x_tab.append(load_words(x_words[1], "x_tab1", X1_AT))
         e_tab = load_words(e_words[0], "e_tab", E_AT)
-        place_scale_rows(e_sc, e_picked, 32, 4, U)
+        place_scale_rows(e_sc, 8, e_picked, 0, 4, U)
         d_tab = load_words(d_words[0], "d_tab", D_AT)
 
         def quantise_w(o, slot):
@@ -174,20 +174,20 @@ def tile_picked_ymmr_mmr_p_kernel(
             hidden_pass(c, 1)
             nc.scalar.copy(h_grouped[c // 2][:, c % 2 * P : (c % 2 + 1) * P, :], acc[c][:].rearrange("p t s -> p s t"))
 
-        h_codes = tile([P, S], U32, "h_codes", H_AT)
+        h_codes = [tile([P, P], U32, "h_codes0"), tile([P, S - P], U32, "h_codes1", H_AT)]
         h_scales = tile([P, S], U8, "h_scales")
-        hq = [(h_codes[:, c * P : (c + 1) * P], h_scales[:, c * P : (c + 1) * P]) for c in range(4)]
+        hq = [(h_codes[0][:], h_scales[:, 0:P])]
+        hq.extend((h_codes[1][:, (c - 1) * P : c * P], h_scales[:, c * P : (c + 1) * P]) for c in range(1, 4))
 
-        def quantise_h(u):
-            cols = slice(u * 2 * P, (u + 1) * 2 * P)
-            nc.vector.quantize_mx(
-                h_codes[:, cols].bitcast(FP8X4), h_scales[:, cols], h_grouped[u][:].rearrange("p s t -> p (s t)")
-            )
+        def quantise_h(codes, c0, c1):
+            values = h_grouped[c0 // 2][:, c0 % 2 * P : (c0 % 2 + c1 - c0) * P, :]
+            nc.vector.quantize_mx(codes.bitcast(FP8X4), h_scales[:, c0 * P : c1 * P], values.rearrange("p s t -> p (s t)"))
 
+        quantise_h(h_codes[0][:], 0, 1)
         e_codes = [gather_seen(0, X1_AT)]
-        quantise_h(0)
+        quantise_h(h_codes[1][:, 0:P], 1, 2)
         e_codes.append(gather_seen(1, E1_AT))
-        quantise_h(1)
+        quantise_h(h_codes[1][:, P : 3 * P], 2, 4)
         res = tile([P, 4, V], F32, "res")
         z = [[bank([P, 2, 2, P], "z%d_%d" % (c, b), Z_BANKS[c][b]) for b in range(2)] for c in range(4)]
         low = [[tile([P, 2, P], F32, "low%d_%d" % (c, i)) for i in range(D)] for c in range(4)]
@@ -198,7 +198,7 @@ def tile_picked_ymmr_mmr_p_kernel(
             nc.tensor.matmul_mx(
                 z[group][b][:, half, :, :].rearrange("p d v -> p (d v)"), lhsT=hq[c][0].bitcast(FP8X4), lhsT_scale=hq[c][1],
                 rhs=e_codes[u][:, 2 * b : 2 * b + 2, :].rearrange("p d v -> p (d v)").bitcast(FP8X4),
-                rhs_scale=e_sc[:, first : first + V], start=True, stop=True,
+                rhs_scale=e_sc[8:P, first : first + V], start=True, stop=True,
             )
 
         def scaled(group, i, out):
@@ -268,14 +268,10 @@ def tile_picked_ymmr_mmr_p_kernel(
         next_seen(1, 3)
         add_scaled(1)
         store(0, 2)
-        next_seen(2, 2)
         next_seen(3, 1)
-        next_seen(2, 3)
-        next_seen(3, 2)
-        score(2, slice(0, V))
-        store(2, 3)
-        for u in range(2):
-            next_seen(3, 3, slice(u, u + 1))
-        for u in range(2):
-            score(3, slice(u * P, (u + 1) * P))
-        store(3, 4)
+        for i in range(2, D):
+            next_seen(2, i)
+            next_seen(3, i)
+        for c in range(2, 4):
+            score(c, slice(0, V))
+            store(c, c + 1)

@@ -87,8 +87,10 @@ def tile_picked_ymmr_mmr_p_kernel(
             return t
 
         xs_tab = tile([P, T], U8, "xs_tab", XS_AT)
-        nc.vector.memset(xs_tab[0:96, :].bitcast(I32), 0)
-        es_tab = zeroed(nc.gpsimd, W, "es_tab", ES_AT)
+        nc.vector.memset(xs_tab[32:64, :].bitcast(I32), 0)
+        nc.vector.memset(xs_tab[64:P, :].bitcast(I32), 0)
+        es_tab = tile([P, W], U8, "es_tab", ES_AT)
+        nc.gpsimd.memset(es_tab[0:112, :].bitcast(I32), 0)
         ds_tab = zeroed(nc.gpsimd, G, "ds_tab", DS_AT)
         x0_sc = zeroed(nc.vector, S, "x0_sc")
         xd_sc = zeroed(nc.vector, S + V, "xd_sc")
@@ -98,26 +100,26 @@ def tile_picked_ymmr_mmr_p_kernel(
 
         w_raw = [tile([P, PACK, H], F32, "w_raw%d" % o) for o in range(2)]
         offs_t = load_list(offs, "offs_t")
-        nc.sync.dma_start(xs_tab[96:P, :].bitcast(I32), x_scales.rearrange("o q n -> (o q) n").bitcast(I32))
+        nc.sync.dma_start(xs_tab[0:32, :].bitcast(I32), x_scales.rearrange("o q n -> (o q) n").bitcast(I32))
+        shown_t = load_list(shown, "shown_t")
+        nc.sync.dma_start(es_tab[112:P, :].bitcast(I32), e_scales[0].bitcast(I32))
         load_w(0, 0, PACK)
         user_t = load_list(user, "user_t")
-        nc.sync.dma_start(ds_tab[112:P, :].bitcast(I32), d_scales[0].bitcast(I32))
-        shown_t = load_list(shown, "shown_t")
-        load_scale_rows(es_tab, 0, e_scales)
+        nc.sync.dma_start(ds_tab[16:32, :].bitcast(I32), d_scales[0].bitcast(I32))
         load_w(1, 0, PACK)
         xd_picked = tile([P, S + V], U8, "xd_picked")
         nc.vector.tensor_copy(xd_picked[:, 0:S], xs_tab[:].indirect(offs_t[:]))
-        nc.vector.tensor_copy(xd_picked[:, S : S + V], ds_tab[:].indirect(user_t[:]))
         e_picked = tile([P, U], U8, "e_picked", PICKED_AT)
         nc.vector.tensor_copy(
             e_picked[:].rearrange("p (u d v) -> p u v d", u=2, d=D), es_tab[:].indirect(shown_t[:])
         )
-        place_scale_rows(x0_sc, 0, xd_picked, 96, 1, S)
+        nc.vector.tensor_copy(xd_picked[:, S : S + V], ds_tab[:].indirect(user_t[:]))
+        place_scale_rows(x0_sc, 0, xd_picked, 0, 1, S)
         x_tab = [load_words(x_words[0], "x_tab0", X0_AT)]
-        place_scale_rows(xd_sc, 4, xd_picked, 112, 1, S + V)
+        place_scale_rows(xd_sc, 4, xd_picked, 16, 1, S + V)
         x_tab.append(load_words(x_words[1], "x_tab1", X1_AT))
         e_tab = load_words(e_words[0], "e_tab", E_AT)
-        place_scale_rows(e_sc, 8, e_picked, 0, 4, U)
+        place_scale_rows(e_sc, 8, e_picked, 112, 1, U)
         d_tab = load_words(d_words[0], "d_tab", D_AT)
 
         def quantise_w(o, slot):
@@ -144,13 +146,13 @@ def tile_picked_ymmr_mmr_p_kernel(
 
         wq = [quantise_w(0, None)]
         x_codes = [tile([P, S], U32, "x_codes0")]
-        gather_pieces(x_codes[0], x_tab[0], (0, 256, 512))
+        gather_pieces(x_codes[0], x_tab[0], (0, 128, 256, 512))
         wq.append(quantise_w(1, X0_AT + 64))
         x_codes.append(tile([P, S], U32, "x_codes1", X0_AT + 64 + H))
         gather_pieces(x_codes[1], x_tab[1], (0, 128, 256, 512))
 
         h_grouped = [tile([P, 2 * P, PACK], BF16, "h_grouped%d" % u) for u in range(2)]
-        acc = [bank([P, PACK, P], "acc%d" % c, 6 + c % 2) for c in range(4)]
+        acc = [bank([P, PACK, P], "acc%d" % c, 4 + c) for c in range(4)]
 
         def hidden_pass(c, o):
             cols = slice(c * P, (c + 1) * P)
@@ -166,11 +168,9 @@ def tile_picked_ymmr_mmr_p_kernel(
                     stop=(o == 1 and t == PACK - 1),
                 )
 
-        for c in range(2):
+        for c in range(4):
             hidden_pass(c, 0)
         for c in range(4):
-            if c >= 2:
-                hidden_pass(c, 0)
             hidden_pass(c, 1)
             nc.scalar.copy(h_grouped[c // 2][:, c % 2 * P : (c % 2 + 1) * P, :], acc[c][:].rearrange("p t s -> p s t"))
 

@@ -19,16 +19,15 @@ P = 128
 PACK = 4
 BANK = 512
 Z_BANKS = ((0, 1), (2, 3), (4, 0), (6, 2))
-XS_AT = 0
+X1_AT = 0
+XS_AT = X1_AT + 4 * T - 64
 X0_AT = XS_AT + T - 64
-DS_AT = X0_AT + 4 * T
-X1_AT = DS_AT + G - 64
-D_AT = X1_AT + 4 * T
+D_AT = X0_AT + 4 * T
 ES_AT = D_AT + 4 * G - 64
 E_AT = ES_AT + W - 64
 H_AT = E_AT + 4 * W
 PICKED_AT = H_AT + 4 * (S - P) - 64
-E1_AT = PICKED_AT + U - 64
+E1_AT = PICKED_AT + U + V - 64
 
 
 def tile_picked_ymmr_mmr_p_kernel(
@@ -91,35 +90,35 @@ def tile_picked_ymmr_mmr_p_kernel(
         nc.vector.memset(xs_tab[64:P, :].bitcast(I32), 0)
         es_tab = tile([P, W], U8, "es_tab", ES_AT)
         nc.gpsimd.memset(es_tab[0:112, :].bitcast(I32), 0)
-        ds_tab = zeroed(nc.gpsimd, G, "ds_tab", DS_AT)
-        x0_sc = zeroed(nc.vector, S, "x0_sc")
-        xd_sc = zeroed(nc.vector, S + V, "xd_sc")
-        x_sc = [x0_sc[:], xd_sc[4:P, 0:S]]
-        d_sc = xd_sc[4:P, S : S + V]
-        e_sc = zeroed(nc.vector, U, "e_sc")
+        ds_tab = zeroed(nc.gpsimd, G, "ds_tab")
+        x_planes = [zeroed(nc.vector, S, "x_plane%d" % o) for o in range(2)]
+        ed_plane = zeroed(nc.vector, U + V, "ed_plane")
+        x_sc = [x_planes[0][:], x_planes[1][4:P, :]]
+        e_sc = ed_plane[8:P, 0:U]
+        d_sc = ed_plane[8:P, U : U + V]
 
         w_raw = [tile([P, PACK, H], F32, "w_raw%d" % o) for o in range(2)]
+        load_w(1, 0, 1)
         offs_t = load_list(offs, "offs_t")
         nc.sync.dma_start(xs_tab[0:32, :].bitcast(I32), x_scales.rearrange("o q n -> (o q) n").bitcast(I32))
         shown_t = load_list(shown, "shown_t")
         nc.sync.dma_start(es_tab[112:P, :].bitcast(I32), e_scales[0].bitcast(I32))
         load_w(0, 0, PACK)
         user_t = load_list(user, "user_t")
-        nc.sync.dma_start(ds_tab[16:32, :].bitcast(I32), d_scales[0].bitcast(I32))
-        load_w(1, 0, PACK)
-        xd_picked = tile([P, S + V], U8, "xd_picked")
-        nc.vector.tensor_copy(xd_picked[:, 0:S], xs_tab[:].indirect(offs_t[:]))
-        e_picked = tile([P, U], U8, "e_picked", PICKED_AT)
+        nc.sync.dma_start(ds_tab[112:P, :].bitcast(I32), d_scales[0].bitcast(I32))
+        load_w(1, 1, PACK)
+        x_picked = gather_bytes(xs_tab, offs_t[:], "x_picked")
+        ed_picked = tile([P, U + V], U8, "ed_picked", PICKED_AT)
         nc.vector.tensor_copy(
-            e_picked[:].rearrange("p (u d v) -> p u v d", u=2, d=D), es_tab[:].indirect(shown_t[:])
+            ed_picked[:, 0:U].rearrange("p (u d v) -> p u v d", u=2, d=D), es_tab[:].indirect(shown_t[:])
         )
-        nc.vector.tensor_copy(xd_picked[:, S : S + V], ds_tab[:].indirect(user_t[:]))
-        place_scale_rows(x0_sc, 0, xd_picked, 0, 1, S)
+        nc.vector.tensor_copy(ed_picked[:, U : U + V], ds_tab[:].indirect(user_t[:]))
+        place_scale_rows(x_planes[0], 0, x_picked, 0, 1, S)
         x_tab = [load_words(x_words[0], "x_tab0", X0_AT)]
-        place_scale_rows(xd_sc, 4, xd_picked, 16, 1, S + V)
+        place_scale_rows(x_planes[1], 4, x_picked, 16, 1, S)
         x_tab.append(load_words(x_words[1], "x_tab1", X1_AT))
         e_tab = load_words(e_words[0], "e_tab", E_AT)
-        place_scale_rows(e_sc, 8, e_picked, 112, 1, U)
+        place_scale_rows(ed_plane, 8, ed_picked, 112, 1, U + V)
         d_tab = load_words(d_words[0], "d_tab", D_AT)
 
         def quantise_w(o, slot):
@@ -198,7 +197,7 @@ def tile_picked_ymmr_mmr_p_kernel(
             nc.tensor.matmul_mx(
                 z[group][b][:, half, :, :].rearrange("p d v -> p (d v)"), lhsT=hq[c][0].bitcast(FP8X4), lhsT_scale=hq[c][1],
                 rhs=e_codes[u][:, 2 * b : 2 * b + 2, :].rearrange("p d v -> p (d v)").bitcast(FP8X4),
-                rhs_scale=e_sc[8:P, first : first + V], start=True, stop=True,
+                rhs_scale=e_sc[:, first : first + V], start=True, stop=True,
             )
 
         def scaled(group, i, out):

@@ -86,11 +86,10 @@ def tile_picked_ymmr_mmr_p_kernel(
             return t
 
         xs_tab = tile([P, T], U8, "xs_tab", XS_AT)
-        nc.vector.memset(xs_tab[32:64, :].bitcast(I32), 0)
-        nc.vector.memset(xs_tab[64:P, :].bitcast(I32), 0)
+        nc.gpsimd.memset(xs_tab[:].bitcast(I32), 0)
         es_tab = tile([P, W], U8, "es_tab", ES_AT)
-        nc.gpsimd.memset(es_tab[0:112, :].bitcast(I32), 0)
-        ds_tab = zeroed(nc.gpsimd, G, "ds_tab")
+        nc.vector.memset(es_tab[:].bitcast(I32), 0)
+        ds_tab = zeroed(nc.vector, G, "ds_tab")
         x_planes = [zeroed(nc.vector, S, "x_plane%d" % o) for o in range(2)]
         ed_plane = zeroed(nc.vector, U + V, "ed_plane")
         x_sc = [x_planes[0][:], x_planes[1][4:P, :]]
@@ -100,12 +99,12 @@ def tile_picked_ymmr_mmr_p_kernel(
         w_raw = [tile([P, PACK, H], F32, "w_raw%d" % o) for o in range(2)]
         load_w(1, 0, 1)
         offs_t = load_list(offs, "offs_t")
-        nc.sync.dma_start(xs_tab[0:32, :].bitcast(I32), x_scales.rearrange("o q n -> (o q) n").bitcast(I32))
         shown_t = load_list(shown, "shown_t")
-        nc.sync.dma_start(es_tab[112:P, :].bitcast(I32), e_scales[0].bitcast(I32))
-        load_w(0, 0, PACK)
+        load_scale_rows(xs_tab, 0, x_scales)
         user_t = load_list(user, "user_t")
-        nc.sync.dma_start(ds_tab[112:P, :].bitcast(I32), d_scales[0].bitcast(I32))
+        load_scale_rows(es_tab, 32, e_scales)
+        load_w(0, 0, PACK)
+        load_scale_rows(ds_tab, 32, d_scales)
         load_w(1, 1, PACK)
         x_picked = gather_bytes(xs_tab, offs_t[:], "x_picked")
         ed_picked = tile([P, U + V], U8, "ed_picked", PICKED_AT)
@@ -113,12 +112,12 @@ def tile_picked_ymmr_mmr_p_kernel(
             ed_picked[:, 0:U].rearrange("p (u d v) -> p u v d", u=2, d=D), es_tab[:].indirect(shown_t[:])
         )
         nc.vector.tensor_copy(ed_picked[:, U : U + V], ds_tab[:].indirect(user_t[:]))
-        place_scale_rows(x_planes[0], 0, x_picked, 0, 1, S)
+        place_scale_rows(x_planes[0], 0, x_picked, 0, 4, S)
         x_tab = [load_words(x_words[0], "x_tab0", X0_AT)]
-        place_scale_rows(x_planes[1], 4, x_picked, 16, 1, S)
+        place_scale_rows(x_planes[1], 4, x_picked, 64, 4, S)
         x_tab.append(load_words(x_words[1], "x_tab1", X1_AT))
         e_tab = load_words(e_words[0], "e_tab", E_AT)
-        place_scale_rows(ed_plane, 8, ed_picked, 112, 1, U + V)
+        place_scale_rows(ed_plane, 8, ed_picked, 32, 4, U + V)
         d_tab = load_words(d_words[0], "d_tab", D_AT)
 
         def quantise_w(o, slot):

@@ -21,10 +21,10 @@ BANK = 512
 Z_BANKS = ((0, 1), (2, 3), (4, 0), (6, 2))
 X1_AT = 0
 XS_AT = X1_AT + 4 * T - 64
-X0_AT = XS_AT + T - 64
-D_AT = X0_AT + 4 * T
-ES_AT = D_AT + 4 * G - 64
-E_AT = ES_AT + W - 64
+E_AT = XS_AT + 2 * T - 64
+X0_AT = E_AT + 4 * W + 8192
+DS_AT = X0_AT + 4 * T
+D_AT = DS_AT + G - 64
 H_AT = E_AT + 4 * W
 PICKED_AT = H_AT + 4 * (S - P) - 64
 E1_AT = PICKED_AT + U + V - 64
@@ -85,39 +85,44 @@ def tile_picked_ymmr_mmr_p_kernel(
             nc.vector.tensor_copy(t[:], table[:].indirect(offsets))
             return t
 
-        xs_tab = tile([P, T], U8, "xs_tab", XS_AT)
-        nc.gpsimd.memset(xs_tab[:].bitcast(I32), 0)
-        es_tab = tile([P, W], U8, "es_tab", ES_AT)
-        nc.vector.memset(es_tab[:].bitcast(I32), 0)
-        ds_tab = zeroed(nc.vector, G, "ds_tab")
-        x_planes = [zeroed(nc.vector, S, "x_plane%d" % o) for o in range(2)]
+        xs_tab = tile([P, 2 * T], U8, "xs_tab", XS_AT)
+        nc.gpsimd.memset(xs_tab[0:112, :].bitcast(I32), 0)
+        es_tab = tile([P, W], U8, "es_tab")
+        ds_tab = tile([P, G], U8, "ds_tab", DS_AT)
+        for t in (es_tab, ds_tab):
+            nc.vector.memset(t[0:48, :].bitcast(I32), 0)
+            nc.vector.memset(t[64:P, :].bitcast(I32), 0)
+        x_plane = zeroed(nc.vector, 2 * S, "x_plane")
         ed_plane = zeroed(nc.vector, U + V, "ed_plane")
-        x_sc = [x_planes[0][:], x_planes[1][4:P, :]]
+        x_sc = [x_plane[:, 0:S], x_plane[:, S : 2 * S]]
         e_sc = ed_plane[8:P, 0:U]
         d_sc = ed_plane[8:P, U : U + V]
 
         w_raw = [tile([P, PACK, H], F32, "w_raw%d" % o) for o in range(2)]
         load_w(1, 0, 1)
         offs_t = load_list(offs, "offs_t")
+        nc.sync.dma_start(
+            xs_tab[112:P, :].bitcast(I32).rearrange("q (o n) -> q o n", o=2), x_scales.bitcast(I32).rearrange("o q n -> q o n")
+        )
         shown_t = load_list(shown, "shown_t")
-        load_scale_rows(xs_tab, 0, x_scales)
-        user_t = load_list(user, "user_t")
-        load_scale_rows(es_tab, 32, e_scales)
+        nc.sync.dma_start(es_tab[48:64, :].bitcast(I32), e_scales[0].bitcast(I32))
         load_w(0, 0, PACK)
-        load_scale_rows(ds_tab, 32, d_scales)
+        user_t = load_list(user, "user_t")
+        nc.sync.dma_start(ds_tab[48:64, :].bitcast(I32), d_scales[0].bitcast(I32))
         load_w(1, 1, PACK)
-        x_picked = gather_bytes(xs_tab, offs_t[:], "x_picked")
+        x_picked = tile([P, 2 * S], U8, "x_picked")
+        for o in range(2):
+            nc.vector.tensor_copy(x_picked[:, o * S : (o + 1) * S], xs_tab[:, o * T : (o + 1) * T].indirect(offs_t[:]))
         ed_picked = tile([P, U + V], U8, "ed_picked", PICKED_AT)
         nc.vector.tensor_copy(
             ed_picked[:, 0:U].rearrange("p (u d v) -> p u v d", u=2, d=D), es_tab[:].indirect(shown_t[:])
         )
         nc.vector.tensor_copy(ed_picked[:, U : U + V], ds_tab[:].indirect(user_t[:]))
-        place_scale_rows(x_planes[0], 0, x_picked, 0, 4, S)
         x_tab = [load_words(x_words[0], "x_tab0", X0_AT)]
-        place_scale_rows(x_planes[1], 4, x_picked, 64, 4, S)
+        place_scale_rows(x_plane, 0, x_picked, 112, 1, 2 * S)
         x_tab.append(load_words(x_words[1], "x_tab1", X1_AT))
         e_tab = load_words(e_words[0], "e_tab", E_AT)
-        place_scale_rows(ed_plane, 8, ed_picked, 32, 4, U + V)
+        place_scale_rows(ed_plane, 8, ed_picked, 48, 1, U + V)
         d_tab = load_words(d_words[0], "d_tab", D_AT)
 
         def quantise_w(o, slot):
@@ -150,7 +155,7 @@ def tile_picked_ymmr_mmr_p_kernel(
         gather_pieces(x_codes[1], x_tab[1], (0, 128, 256, 512))
 
         h_grouped = [tile([P, 2 * P, PACK], BF16, "h_grouped%d" % u) for u in range(2)]
-        acc = [bank([P, PACK, P], "acc%d" % c, 4 + c) for c in range(4)]
+        acc = [bank([P, PACK, P], "acc%d" % c, 4 + c % 3) for c in range(4)]
 
         def hidden_pass(c, o):
             cols = slice(c * P, (c + 1) * P)
@@ -166,9 +171,11 @@ def tile_picked_ymmr_mmr_p_kernel(
                     stop=(o == 1 and t == PACK - 1),
                 )
 
-        for c in range(4):
+        for c in range(3):
             hidden_pass(c, 0)
         for c in range(4):
+            if c == 3:
+                hidden_pass(c, 0)
             hidden_pass(c, 1)
             nc.scalar.copy(h_grouped[c // 2][:, c % 2 * P : (c % 2 + 1) * P, :], acc[c][:].rearrange("p t s -> p s t"))
 

@@ -99,17 +99,16 @@ def tile_picked_ymmr_mmr_p_kernel(
         d_sc = ed_plane[8:P, U : U + V]
 
         w_raw = [tile([P, PACK, H], F32, "w_raw%d" % o) for o in range(2)]
-        load_w(1, 0, 1)
-        offs_t = load_list(offs, "offs_t")
         nc.sync.dma_start(
             xs_tab[112:P, :].bitcast(I32).rearrange("q (o n) -> q o n", o=2), x_scales.bitcast(I32).rearrange("o q n -> q o n")
         )
-        shown_t = load_list(shown, "shown_t")
+        offs_t = load_list(offs, "offs_t")
         nc.sync.dma_start(es_tab[48:64, :].bitcast(I32), e_scales[0].bitcast(I32))
+        shown_t = load_list(shown, "shown_t")
         load_w(0, 0, PACK)
         user_t = load_list(user, "user_t")
         nc.sync.dma_start(ds_tab[48:64, :].bitcast(I32), d_scales[0].bitcast(I32))
-        load_w(1, 1, PACK)
+        load_w(1, 0, PACK)
         x_picked = tile([P, 2 * S], U8, "x_picked")
         for o in range(2):
             nc.vector.tensor_copy(x_picked[:, o * S : (o + 1) * S], xs_tab[:, o * T : (o + 1) * T].indirect(offs_t[:]))

@@ -147,6 +147,12 @@ def tile_picked_ymmr_mmr_p_kernel(
             return t
 
         wq = [quantise_w(0, None)]
+        warm = bank([P, BANK], "warm", 7)
+        for width in (BANK, V):
+            nc.tensor.matmul_mx(
+                warm[:, 0:width], lhsT=wq[0][0][:, 0:P].bitcast(FP8X4), lhsT_scale=wq[0][1][:, 0:P],
+                rhs=wq[0][0][:, 0:width].bitcast(FP8X4), rhs_scale=wq[0][1][:, 0:width], start=True, stop=True,
+            )
         x_codes = [tile([P, S], U32, "x_codes0")]
         gather_pieces(x_codes[0], x_tab[0], (0, 128, 256, 512))
         wq.append(quantise_w(1, X0_AT + 64))

@@ -28,6 +28,7 @@ D_AT = DS_AT + G - 64
 H_AT = E_AT + 4 * W
 PICKED_AT = H_AT + 4 * (S - P) - 64
 E1_AT = PICKED_AT + U + V - 64
+X_PICKED_AT = D_AT + 4 * G
 
 
 def tile_picked_ymmr_mmr_p_kernel(
@@ -109,7 +110,7 @@ def tile_picked_ymmr_mmr_p_kernel(
         user_t = load_list(user, "user_t")
         nc.sync.dma_start(ds_tab[48:64, :].bitcast(I32), d_scales[0].bitcast(I32))
         load_w(1, 0, PACK)
-        x_picked = tile([P, 2 * S], U8, "x_picked")
+        x_picked = tile([P, 2 * S], U8, "x_picked", X_PICKED_AT)
         for o in range(2):
             nc.vector.tensor_copy(x_picked[:, o * S : (o + 1) * S], xs_tab[:, o * T : (o + 1) * T].indirect(offs_t[:]))
         ed_picked = tile([P, U + V], U8, "ed_picked", PICKED_AT)
@@ -155,8 +156,8 @@ def tile_picked_ymmr_mmr_p_kernel(
             )
         x_codes = [tile([P, S], U32, "x_codes0")]
         gather_pieces(x_codes[0], x_tab[0], (0, 128, 256, 512))
-        wq.append(quantise_w(1, X0_AT + 64))
-        x_codes.append(tile([P, S], U32, "x_codes1", X0_AT + 64 + H))
+        wq.append(quantise_w(1, X_PICKED_AT))
+        x_codes.append(tile([P, S], U32, "x_codes1"))
         gather_pieces(x_codes[1], x_tab[1], (0, 128, 256, 512))
 
         h_grouped = [tile([P, 2 * P, PACK], BF16, "h_grouped%d" % u) for u in range(2)]

@@ -20,14 +20,15 @@ PACK = 4
 BANK = 512
 Z_BANKS = ((0, 1), (2, 3), (4, 0), (6, 2))
 X1_AT = 0
-XS_AT = X1_AT + 4 * T - 64
-E_AT = XS_AT + 2 * T - 64
+ALIGN = 256
+XS_AT = X1_AT + 4 * T - ALIGN
+E_AT = XS_AT + 2 * T - ALIGN
 X0_AT = E_AT + 4 * W + 8192
 DS_AT = X0_AT + 4 * T
-D_AT = DS_AT + G - 64
+D_AT = DS_AT + G - ALIGN
 H_AT = E_AT + 4 * W
-PICKED_AT = H_AT + 4 * (S - P) - 64
-E1_AT = PICKED_AT + U + V - 64
+PICKED_AT = H_AT + 4 * (S - P) - ALIGN
+E1_AT = PICKED_AT + U + V - ALIGN
 X_PICKED_AT = D_AT + 4 * G
 
 
@@ -45,8 +46,8 @@ def tile_picked_ymmr_mmr_p_kernel(
 
         def tile(shape, dtype, name, slot=None):
             if isinstance(slot, int):
-                return reuse.tile(shape, dtype, name=name, align_bytes=64, offset=slot)
-            return keep.tile(shape, dtype, name=name, tag=slot or name, align_bytes=64)
+                return reuse.tile(shape, dtype, name=name, align_bytes=ALIGN, offset=slot)
+            return keep.tile(shape, dtype, name=name, tag=slot or name, align_bytes=ALIGN)
 
         def load_list(src, name):
             t = keep.tile(list(src.shape), U16, name=name)

@@ -19,17 +19,19 @@ P = 128
 PACK = 4
 BANK = 512
 Z_BANKS = ((0, 1), (2, 3), (4, 0), (6, 2))
-X1_AT = 0
 ALIGN = 256
-XS_AT = X1_AT + 4 * T - ALIGN
-E_AT = XS_AT + 2 * T - ALIGN
-X0_AT = E_AT + 4 * W + 8192
-DS_AT = X0_AT + 4 * T
-D_AT = DS_AT + G - ALIGN
-H_AT = E_AT + 4 * W
+PAGE = 4096
+X1_AT = 0
+E_AT = X1_AT + 4 * T
+XS_AT = E_AT - T
+X0_AT = E_AT + 4 * W
+D_AT = X0_AT + 4 * T
+DS_AT = D_AT
+W_AT = D_AT + 4 * G
+H_AT = W_AT + 2 * 4 * PACK * H
 PICKED_AT = H_AT + 4 * (S - P) - ALIGN
 E1_AT = PICKED_AT + U + V - ALIGN
-X_PICKED_AT = D_AT + 4 * G
+X_PICKED_AT = E1_AT + 4 * BANK
 
 
 def tile_picked_ymmr_mmr_p_kernel(
@@ -46,7 +48,7 @@ def tile_picked_ymmr_mmr_p_kernel(
 
         def tile(shape, dtype, name, slot=None):
             if isinstance(slot, int):
-                return reuse.tile(shape, dtype, name=name, align_bytes=ALIGN, offset=slot)
+                return reuse.tile(shape, dtype, name=name, align_bytes=ALIGN if slot % PAGE else PAGE, offset=slot)
             return keep.tile(shape, dtype, name=name, tag=slot or name, align_bytes=ALIGN)
 
         def load_list(src, name):
@@ -100,7 +102,7 @@ def tile_picked_ymmr_mmr_p_kernel(
         e_sc = ed_plane[8:P, 0:U]
         d_sc = ed_plane[8:P, U : U + V]
 
-        w_raw = [tile([P, PACK, H], F32, "w_raw%d" % o) for o in range(2)]
+        w_raw = [tile([P, PACK, H], F32, "w_raw%d" % o, W_AT + o * 4 * PACK * H) for o in range(2)]
         nc.sync.dma_start(
             xs_tab[112:P, :].bitcast(I32).rearrange("q (o n) -> q o n", o=2), x_scales.bitcast(I32).rearrange("o q n -> q o n")
         )

@@ -186,7 +186,10 @@ def tile_picked_ymmr_mmr_p_kernel(
             if c == 3:
                 hidden_pass(c, 0)
             hidden_pass(c, 1)
-            nc.scalar.copy(h_grouped[c // 2][:, c % 2 * P : (c % 2 + 1) * P, :], acc[c][:].rearrange("p t s -> p s t"))
+            for a, b in ((0, 64), (64, P)) if c == 0 else ((0, P),):
+                nc.scalar.copy(
+                    h_grouped[c // 2][:, c % 2 * P + a : c % 2 * P + b, :], acc[c][:, :, a:b].rearrange("p t s -> p s t")
+                )
 
         h_codes = [tile([P, P], U32, "h_codes0"), tile([P, S - P], U32, "h_codes1", H_AT)]
         h_scales = tile([P, S], U8, "h_scales")
@@ -197,7 +200,11 @@ def tile_picked_ymmr_mmr_p_kernel(
             values = h_grouped[c0 // 2][:, c0 % 2 * P : (c0 % 2 + c1 - c0) * P, :]
             nc.vector.quantize_mx(codes.bitcast(FP8X4), h_scales[:, c0 * P : c1 * P], values.rearrange("p s t -> p (s t)"))
 
-        quantise_h(h_codes[0][:], 0, 1)
+        for a in (0, 64):
+            nc.vector.quantize_mx(
+                h_codes[0][:, a : a + 64].bitcast(FP8X4), h_scales[:, a : a + 64],
+                h_grouped[0][:, a : a + 64, :].rearrange("p s t -> p (s t)"),
+            )
         e_codes = [gather_seen(0, X1_AT)]
         quantise_h(h_codes[1][:, 0:P], 1, 2)
         e_codes.append(gather_seen(1, E1_AT))

@@ -18,7 +18,8 @@ COPY = mybir.ActivationFunctionType.Copy
 P = 128
 PACK = 4
 BANK = 512
-Z_BANKS = ((0, 1), (2, 3), (4, 0), (6, 2))
+Z_BANKS = ((0, 1), (2, 3), (4, 1), (6, 0))
+CHAIN = (0, 2, 1, 3)
 ALIGN = 256
 PAGE = 4096
 X1_AT = 0
@@ -96,8 +97,8 @@ def tile_picked_ymmr_mmr_p_kernel(
         for t in (es_tab, ds_tab):
             nc.vector.memset(t[0:48, :].bitcast(I32), 0)
             nc.vector.memset(t[64:P, :].bitcast(I32), 0)
-        x_plane = zeroed(nc.vector, 2 * S, "x_plane")
-        ed_plane = zeroed(nc.vector, U + V, "ed_plane")
+        planes = zeroed(nc.vector, 2 * S + U + V, "planes")
+        x_plane, ed_plane = planes[:, 0 : 2 * S], planes[:, 2 * S :]
         x_sc = [x_plane[:, 0:S], x_plane[:, S : 2 * S]]
         e_sc = ed_plane[8:P, 0:U]
         d_sc = ed_plane[8:P, U : U + V]
@@ -205,7 +206,7 @@ def tile_picked_ymmr_mmr_p_kernel(
                 h_codes[0][:, a : a + 64].bitcast(FP8X4), h_scales[:, a : a + 64],
                 h_grouped[0][:, a : a + 64, :].rearrange("p s t -> p (s t)"),
             )
-        e_codes = [gather_seen(0, X1_AT)]
+        e_codes = [gather_seen(0, None)]
         quantise_h(h_codes[1][:, 0:P], 1, 2)
         e_codes.append(gather_seen(1, E1_AT))
         quantise_h(h_codes[1][:, P : 3 * P], 2, 4)
@@ -231,7 +232,7 @@ def tile_picked_ymmr_mmr_p_kernel(
             )
 
         def next_seen(group, i, half=slice(0, 2)):
-            lower(group, i, low[group][i], low[group][i - 1], half)
+            lower(group, CHAIN[i] if group == 1 else i, low[group][i], low[group][i - 1], half)
 
         def intent(pair):
             y = bank([P, 2, V], "y%d" % pair, 5 + 2 * pair)
@@ -260,7 +261,7 @@ def tile_picked_ymmr_mmr_p_kernel(
             for b in range(2):
                 seen(0, u, b)
                 seen(1, u, b)
-        d_codes = gather(d_tab, user_t[:], U32, "d_codes", E_AT)
+        d_codes = gather(d_tab, user_t[:], U32, "d_codes")
         third = tile([P, 2, P], F32, "third")
         scaled(0, 0, low[0][0])
         scaled(0, 2, third)
@@ -275,13 +276,13 @@ def tile_picked_ymmr_mmr_p_kernel(
         seen(3, 1, 0)
         scaled(3, 0, low[3][0])
         nc.scalar.activation(y_scaled[1][:], y[0][:, :, P:V], COPY, scale=0.7)
-        next_seen(0, 1)
+        lower(0, 1, low[0][1], low[0][0])
         lower(0, 3, low[0][2], third)
-        next_seen(1, 1)
-        for c in range(2, 4):
+        y.append(intent(1))
+        for c in (3, 2):
             seen(c, 0, 1)
             seen(c, 1, 1)
-        y.append(intent(1))
+        next_seen(1, 1)
         nc.vector.tensor_tensor(low[0][3][:], low[0][1][:], low[0][2][:], ALU.min)
         add_scaled(0)
         next_seen(1, 2)

@@ -253,6 +253,7 @@ def tile_picked_ymmr_mmr_p_kernel(
         def add_scaled(u):
             users = slice(u * P, (u + 1) * P)
             nc.gpsimd.tensor_tensor(res[:, 0:2, users], y_scaled[u][:], low[u][D - 1][:], ALU.add)
+            nc.sync.dma_start(out[0 : 2 * P, users].rearrange("(c p) v -> p c v", p=P), res[:, 0:2, users])
 
         def score(c, users):
             nc.vector.scalar_tensor_tensor(res[:, c, users], y[1][:, c - 2, users], 0.7, nearest(c)[:, users], ALU.mult, ALU.add)
@@ -289,7 +290,6 @@ def tile_picked_ymmr_mmr_p_kernel(
         next_seen(2, 1)
         next_seen(1, 3)
         add_scaled(1)
-        store(0, 2)
         next_seen(3, 1)
         for i in range(2, D):
             next_seen(2, i)

@@ -18,8 +18,18 @@ COPY = mybir.ActivationFunctionType.Copy
 P = 128
 PACK = 4
 BANK = 512
+RELEVANCE, REDUNDANCY = 0.7, -0.3
+
+X_ROWS, ED_ROWS = 112, 48
+ED_FIRST = 8
+X_PIECES = (0, 128, 256, 512)
+HALF_CHUNK = 64
+
 Z_BANKS = ((0, 1), (2, 3), (4, 1), (6, 0))
-CHAIN = (0, 2, 1, 3)
+H_BANKS = (4, 5, 6, 4)
+Y_BANKS = (5, 7)
+CHAINS = {1: (0, 2, 1, 3), 2: (0, 1, 2, 3), 3: (0, 1, 2, 3)}
+
 ALIGN = 256
 PAGE = 4096
 X1_AT = 0
@@ -47,73 +57,62 @@ def tile_picked_ymmr_mmr_p_kernel(
         def bank(shape, name, number):
             return psum.tile(shape, F32, name=name, tag="bank%d" % number)
 
-        def tile(shape, dtype, name, slot=None):
-            if isinstance(slot, int):
-                return reuse.tile(shape, dtype, name=name, align_bytes=ALIGN if slot % PAGE else PAGE, offset=slot)
-            return keep.tile(shape, dtype, name=name, tag=slot or name, align_bytes=ALIGN)
+        def tile(shape, dtype, name, at=None):
+            if at is None:
+                return keep.tile(shape, dtype, name=name, tag=name, align_bytes=ALIGN)
+            return reuse.tile(shape, dtype, name=name, align_bytes=ALIGN if at % PAGE else PAGE, offset=at)
 
         def load_list(src, name):
             t = keep.tile(list(src.shape), U16, name=name)
             nc.sync.dma_start(t[:], src)
             return t
 
-        def load_words(src, name, slot=None):
-            t = tile([P, src.shape[1]], I32, name, slot)
+        def load_words(src, name, at):
+            t = tile([P, src.shape[1]], I32, name, at)
             nc.sync.dma_start(t[:], src.rearrange("p n r -> p (n r)").bitcast(I32))
             return t
 
-        def zeroed(engine, width, name, slot=None):
-            t = tile([P, width], U8, name, slot)
-            engine.memset(t[:].bitcast(I32), 0)
-            return t
+        def load_w(o):
+            nc.sync.dma_start(w_raw[o][:], w1[o * 512 : (o + 1) * 512, :].rearrange("(p j) c -> p j c", j=PACK))
 
-        def load_scale_rows(t, first, src):
-            rows = src.rearrange("o q n -> (o q) n")
-            nc.sync.dma_start(t[first : first + 4 * rows.shape[0] : 4, :].bitcast(I32), rows.bitcast(I32))
-
-        def place_scale_rows(plane, row, picked, first, step, width):
+        def move_scale_rows(planes, first, picked, rows):
             for r in range(4):
-                src = picked[first + step * r : first + 16 * step : 4 * step, 0:width]
-                nc.sync.dma_start(plane[row + r : P : 32, :].bitcast(I32), src.bitcast(I32))
+                src = picked[rows + r : rows + 16 : 4, :]
+                nc.sync.dma_start(planes[first + r : P : 32, :].bitcast(I32), src.bitcast(I32))
 
-        def load_w(o, j0, j1):
-            rows = w1[o * 512 : (o + 1) * 512, :].rearrange("(p j) c -> p j c", j=PACK)
-            nc.sync.dma_start(w_raw[o][:, j0:j1, :], rows[:, j0:j1, :])
-
-        def gather(table, offsets, dtype, name, slot=None):
-            t = tile([P, 16 * offsets.shape[1]], dtype, name, slot)
-            nc.vector.tensor_copy(t[:], table[:].bitcast(dtype).indirect(offsets))
-            return t
-
-        def gather_bytes(table, offsets, name, slot=None):
-            t = tile([P, 16 * offsets.shape[1]], U8, name, slot)
-            nc.vector.tensor_copy(t[:], table[:].indirect(offsets))
-            return t
+        def product(acc, lhs, lhs_scales, rhs, rhs_scales, start=True, stop=True):
+            nc.tensor.matmul_mx(
+                acc, lhsT=lhs.bitcast(FP8X4), lhsT_scale=lhs_scales, rhs=rhs.bitcast(FP8X4), rhs_scale=rhs_scales,
+                start=start, stop=stop,
+            )
 
         xs_tab = tile([P, 2 * T], U8, "xs_tab", XS_AT)
-        nc.gpsimd.memset(xs_tab[0:112, :].bitcast(I32), 0)
+        nc.gpsimd.memset(xs_tab[0:X_ROWS, :].bitcast(I32), 0)
         es_tab = tile([P, W], U8, "es_tab")
         ds_tab = tile([P, G], U8, "ds_tab", DS_AT)
         for t in (es_tab, ds_tab):
-            nc.vector.memset(t[0:48, :].bitcast(I32), 0)
-            nc.vector.memset(t[64:P, :].bitcast(I32), 0)
-        planes = zeroed(nc.vector, 2 * S + U + V, "planes")
-        x_plane, ed_plane = planes[:, 0 : 2 * S], planes[:, 2 * S :]
-        x_sc = [x_plane[:, 0:S], x_plane[:, S : 2 * S]]
-        e_sc = ed_plane[8:P, 0:U]
-        d_sc = ed_plane[8:P, U : U + V]
+            nc.vector.memset(t[0:ED_ROWS, :].bitcast(I32), 0)
+            nc.vector.memset(t[ED_ROWS + 16 : P, :].bitcast(I32), 0)
+        moved = tile([P, 2 * S + U + V], U8, "planes")
+        nc.vector.memset(moved[:].bitcast(I32), 0)
+        x_moved, ed_moved = moved[:, 0 : 2 * S], moved[:, 2 * S :]
+        x_sc = [x_moved[:, 0:S], x_moved[:, S : 2 * S]]
+        e_sc = ed_moved[ED_FIRST:P, 0:U]
+        d_sc = ed_moved[ED_FIRST:P, U : U + V]
 
         w_raw = [tile([P, PACK, H], F32, "w_raw%d" % o, W_AT + o * 4 * PACK * H) for o in range(2)]
         nc.sync.dma_start(
-            xs_tab[112:P, :].bitcast(I32).rearrange("q (o n) -> q o n", o=2), x_scales.bitcast(I32).rearrange("o q n -> q o n")
+            xs_tab[X_ROWS:P, :].bitcast(I32).rearrange("q (o n) -> q o n", o=2),
+            x_scales.bitcast(I32).rearrange("o q n -> q o n"),
         )
         offs_t = load_list(offs, "offs_t")
-        nc.sync.dma_start(es_tab[48:64, :].bitcast(I32), e_scales[0].bitcast(I32))
+        nc.sync.dma_start(es_tab[ED_ROWS : ED_ROWS + 16, :].bitcast(I32), e_scales[0].bitcast(I32))
         shown_t = load_list(shown, "shown_t")
-        load_w(0, 0, PACK)
+        load_w(0)
         user_t = load_list(user, "user_t")
-        nc.sync.dma_start(ds_tab[48:64, :].bitcast(I32), d_scales[0].bitcast(I32))
-        load_w(1, 0, PACK)
+        nc.sync.dma_start(ds_tab[ED_ROWS : ED_ROWS + 16, :].bitcast(I32), d_scales[0].bitcast(I32))
+        load_w(1)
+
         x_picked = tile([P, 2 * S], U8, "x_picked", X_PICKED_AT)
         for o in range(2):
             nc.vector.tensor_copy(x_picked[:, o * S : (o + 1) * S], xs_tab[:, o * T : (o + 1) * T].indirect(offs_t[:]))
@@ -122,178 +121,169 @@ def tile_picked_ymmr_mmr_p_kernel(
             ed_picked[:, 0:U].rearrange("p (u d v) -> p u v d", u=2, d=D), es_tab[:].indirect(shown_t[:])
         )
         nc.vector.tensor_copy(ed_picked[:, U : U + V], ds_tab[:].indirect(user_t[:]))
+
         x_tab = [load_words(x_words[0], "x_tab0", X0_AT)]
-        place_scale_rows(x_plane, 0, x_picked, 112, 1, 2 * S)
+        move_scale_rows(x_moved, 0, x_picked, X_ROWS)
         x_tab.append(load_words(x_words[1], "x_tab1", X1_AT))
         e_tab = load_words(e_words[0], "e_tab", E_AT)
-        place_scale_rows(ed_plane, 8, ed_picked, 48, 1, U + V)
+        move_scale_rows(ed_moved, ED_FIRST, ed_picked, ED_ROWS)
         d_tab = load_words(d_words[0], "d_tab", D_AT)
 
-        def quantise_w(o, slot):
+        def quantise_w(o, scales_at):
             grouped = tile([P, PACK * H], BF16, "w_grouped%d" % o)
             nc.scalar.copy(
-                grouped[:].rearrange("p (t m j) -> p m t j", t=4, j=PACK),
-                w_raw[o][:].rearrange("p j (m t) -> p m t j", t=4),
+                grouped[:].rearrange("p (t m j) -> p m t j", t=PACK, j=PACK),
+                w_raw[o][:].rearrange("p j (m t) -> p m t j", t=PACK),
             )
             codes = tile([P, H], U32, "w_codes%d" % o)
-            scales = tile([P, H], U8, "w_scales%d" % o, slot)
+            scales = tile([P, H], U8, "w_scales%d" % o, scales_at)
             nc.vector.quantize_mx(codes[:].bitcast(FP8X4), scales[:], grouped[:])
             return codes, scales
 
-        def gather_pieces(t, table, edges):
-            for a, b in zip(edges, edges[1:]):
-                nc.vector.tensor_copy(t[:, a:b], table[:].bitcast(U32).indirect(offs_t[:, a // 16 : b // 16]))
+        def gather_x(o):
+            t = tile([P, S], U32, "x_codes%d" % o)
+            for a, b in zip(X_PIECES, X_PIECES[1:]):
+                nc.vector.tensor_copy(t[:, a:b], x_tab[o][:].bitcast(U32).indirect(offs_t[:, a // 16 : b // 16]))
+            return t
 
-        def gather_seen(u, slot):
-            t = tile([P, D, P], U32, "e_codes%d" % u, slot)
+        def gather_seen(u, at):
+            t = tile([P, D, P], U32, "e_codes%d" % u, at)
             nc.vector.tensor_copy(
                 t[:].rearrange("p d v -> p v d"), e_tab[:].bitcast(U32).indirect(shown_t[:, 32 * u : 32 * (u + 1)])
             )
             return t
 
         wq = [quantise_w(0, None)]
-        warm = bank([P, BANK], "warm", 7)
-        for width in (BANK, V):
-            nc.tensor.matmul_mx(
-                warm[:, 0:width], lhsT=wq[0][0][:, 0:P].bitcast(FP8X4), lhsT_scale=wq[0][1][:, 0:P],
-                rhs=wq[0][0][:, 0:width].bitcast(FP8X4), rhs_scale=wq[0][1][:, 0:width], start=True, stop=True,
-            )
-        x_codes = [tile([P, S], U32, "x_codes0")]
-        gather_pieces(x_codes[0], x_tab[0], (0, 128, 256, 512))
+        x_codes = [gather_x(0)]
         wq.append(quantise_w(1, X_PICKED_AT))
-        x_codes.append(tile([P, S], U32, "x_codes1"))
-        gather_pieces(x_codes[1], x_tab[1], (0, 128, 256, 512))
+        x_codes.append(gather_x(1))
 
-        h_grouped = [tile([P, 2 * P, PACK], BF16, "h_grouped%d" % u) for u in range(2)]
-        acc = [bank([P, PACK, P], "acc%d" % c, 4 + c % 3) for c in range(4)]
+        h_grouped = [tile([P, 2 * P, PACK], BF16, "h_grouped%d" % pair) for pair in range(2)]
+        acc = [bank([P, PACK, P], "acc%d" % c, H_BANKS[c]) for c in range(4)]
 
         def hidden_pass(c, o):
             cols = slice(c * P, (c + 1) * P)
             for t in range(PACK):
                 ch = slice(t * P, (t + 1) * P)
-                nc.tensor.matmul_mx(
-                    acc[c][:, t, :],
-                    lhsT=wq[o][0][:, ch].bitcast(FP8X4),
-                    lhsT_scale=wq[o][1][:, ch],
-                    rhs=x_codes[o][:, cols].bitcast(FP8X4),
-                    rhs_scale=x_sc[o][:, cols],
-                    start=(o == 0 and t == 0),
-                    stop=(o == 1 and t == PACK - 1),
+                product(
+                    acc[c][:, t, :], wq[o][0][:, ch], wq[o][1][:, ch], x_codes[o][:, cols], x_sc[o][:, cols],
+                    start=(o == 0 and t == 0), stop=(o == 1 and t == PACK - 1),
                 )
+
+        def round_h(c, a, b):
+            at = c % 2 * P
+            nc.scalar.copy(h_grouped[c // 2][:, at + a : at + b, :], acc[c][:, :, a:b].rearrange("p t s -> p s t"))
 
         for c in range(3):
             hidden_pass(c, 0)
-        for c in range(4):
-            if c == 3:
-                hidden_pass(c, 0)
+        hidden_pass(0, 1)
+        round_h(0, 0, HALF_CHUNK)
+        round_h(0, HALF_CHUNK, P)
+        for c in (1, 2):
             hidden_pass(c, 1)
-            for a, b in ((0, 64), (64, P)) if c == 0 else ((0, P),):
-                nc.scalar.copy(
-                    h_grouped[c // 2][:, c % 2 * P + a : c % 2 * P + b, :], acc[c][:, :, a:b].rearrange("p t s -> p s t")
-                )
+            round_h(c, 0, P)
+        hidden_pass(3, 0)
+        hidden_pass(3, 1)
+        round_h(3, 0, P)
 
-        h_codes = [tile([P, P], U32, "h_codes0"), tile([P, S - P], U32, "h_codes1", H_AT)]
+        h_first = tile([P, P], U32, "h_codes0")
+        h_rest = tile([P, S - P], U32, "h_codes1", H_AT)
         h_scales = tile([P, S], U8, "h_scales")
-        hq = [(h_codes[0][:], h_scales[:, 0:P])]
-        hq.extend((h_codes[1][:, (c - 1) * P : c * P], h_scales[:, c * P : (c + 1) * P]) for c in range(1, 4))
+        hq = [(h_first[:], h_scales[:, 0:P])]
+        hq.extend((h_rest[:, (c - 1) * P : c * P], h_scales[:, c * P : (c + 1) * P]) for c in range(1, 4))
 
-        def quantise_h(codes, c0, c1):
-            values = h_grouped[c0 // 2][:, c0 % 2 * P : (c0 % 2 + c1 - c0) * P, :]
-            nc.vector.quantize_mx(codes.bitcast(FP8X4), h_scales[:, c0 * P : c1 * P], values.rearrange("p s t -> p (s t)"))
+        def quantise_h(codes, a, b):
+            values = h_grouped[a // (2 * P)][:, a % (2 * P) : a % (2 * P) + b - a, :]
+            nc.vector.quantize_mx(codes.bitcast(FP8X4), h_scales[:, a:b], values.rearrange("p s t -> p (s t)"))
 
-        for a in (0, 64):
-            nc.vector.quantize_mx(
-                h_codes[0][:, a : a + 64].bitcast(FP8X4), h_scales[:, a : a + 64],
-                h_grouped[0][:, a : a + 64, :].rearrange("p s t -> p (s t)"),
-            )
+        quantise_h(h_first[:, 0:HALF_CHUNK], 0, HALF_CHUNK)
+        quantise_h(h_first[:, HALF_CHUNK:P], HALF_CHUNK, P)
         e_codes = [gather_seen(0, None)]
-        quantise_h(h_codes[1][:, 0:P], 1, 2)
+        quantise_h(h_rest[:, 0:P], P, 2 * P)
         e_codes.append(gather_seen(1, E1_AT))
-        quantise_h(h_codes[1][:, P : 3 * P], 2, 4)
+        quantise_h(h_rest[:, P : 3 * P], 2 * P, S)
+
         res = tile([P, 4, V], F32, "res")
-        z = [[bank([P, 2, 2, P], "z%d_%d" % (c, b), Z_BANKS[c][b]) for b in range(2)] for c in range(4)]
-        low = [[tile([P, 2, P], F32, "low%d_%d" % (c, i)) for i in range(D)] for c in range(4)]
+        z = [[bank([P, 2, 2, P], "z%d_%d" % (g, b), Z_BANKS[g][b]) for b in range(2)] for g in range(4)]
+        low = [[tile([P, 2, P], F32, "low%d_%d" % (g, i)) for i in range(D)] for g in range(4)]
 
         def seen(c, u, b):
             group, half = (u, c) if c < 2 else (c, u)
             first = u * BANK + b * V
-            nc.tensor.matmul_mx(
-                z[group][b][:, half, :, :].rearrange("p d v -> p (d v)"), lhsT=hq[c][0].bitcast(FP8X4), lhsT_scale=hq[c][1],
-                rhs=e_codes[u][:, 2 * b : 2 * b + 2, :].rearrange("p d v -> p (d v)").bitcast(FP8X4),
-                rhs_scale=e_sc[:, first : first + V], start=True, stop=True,
+            product(
+                z[group][b][:, half, :, :].rearrange("p d v -> p (d v)"), hq[c][0], hq[c][1],
+                e_codes[u][:, 2 * b : 2 * b + 2, :].rearrange("p d v -> p (d v)"), e_sc[:, first : first + V],
             )
 
-        def scaled(group, i, out):
-            nc.scalar.activation(out[:], z[group][i // 2][:, :, i % 2, :], COPY, scale=-0.3)
-
-        def lower(group, i, out, prior, half=slice(0, 2)):
-            nc.vector.scalar_tensor_tensor(
-                out[:, half, :], z[group][i // 2][:, half, i % 2, :], -0.3, prior[:, half, :], ALU.mult, ALU.min
-            )
-
-        def next_seen(group, i, half=slice(0, 2)):
-            lower(group, CHAIN[i] if group == 1 else i, low[group][i], low[group][i - 1], half)
+        def seen_by_all(c, b):
+            for u in range(2):
+                seen(c, u, b)
 
         def intent(pair):
-            y = bank([P, 2, V], "y%d" % pair, 5 + 2 * pair)
+            y_pair = bank([P, 2, V], "y%d" % pair, Y_BANKS[pair])
             for i in range(2):
-                codes, scales = hq[2 * pair + i]
-                nc.tensor.matmul_mx(
-                    y[:, i, :], lhsT=codes.bitcast(FP8X4), lhsT_scale=scales,
-                    rhs=d_codes[:].bitcast(FP8X4), rhs_scale=d_sc, start=True, stop=True,
-                )
-            return y
+                product(y_pair[:, i, :], hq[2 * pair + i][0], hq[2 * pair + i][1], d_codes[:], d_sc)
+            return y_pair
 
-        def nearest(c):
-            return low[c][D - 1][:].rearrange("p u v -> p (u v)")
+        def open_with(group, item, dst):
+            nc.scalar.activation(dst[:], z[group][item // 2][:, :, item % 2, :], COPY, scale=REDUNDANCY)
 
-        def store(c0, c1):
-            nc.sync.dma_start(out[c0 * P : c1 * P, :].rearrange("(c p) v -> p c v", p=P), res[:, c0:c1, :])
+        def lower(group, item, dst, prior):
+            nc.vector.scalar_tensor_tensor(
+                dst[:], z[group][item // 2][:, :, item % 2, :], REDUNDANCY, prior[:], ALU.mult, ALU.min
+            )
 
-        def add_scaled(u):
+        def step(group, i):
+            lower(group, CHAINS[group][i], low[group][i], low[group][i - 1])
+
+        def scale_intent(u):
+            nc.scalar.activation(y_scaled[u][:], y[0][:, :, u * P : (u + 1) * P], COPY, scale=RELEVANCE)
+
+        def finish_on_gpsimd(u):
             users = slice(u * P, (u + 1) * P)
             nc.gpsimd.tensor_tensor(res[:, 0:2, users], y_scaled[u][:], low[u][D - 1][:], ALU.add)
             nc.sync.dma_start(out[0 : 2 * P, users].rearrange("(c p) v -> p c v", p=P), res[:, 0:2, users])
 
-        def score(c, users):
-            nc.vector.scalar_tensor_tensor(res[:, c, users], y[1][:, c - 2, users], 0.7, nearest(c)[:, users], ALU.mult, ALU.add)
+        def finish_on_vector(c):
+            nearest = low[c][D - 1][:].rearrange("p u v -> p (u v)")
+            nc.vector.scalar_tensor_tensor(res[:, c, :], y[1][:, c - 2, :], RELEVANCE, nearest, ALU.mult, ALU.add)
+            nc.sync.dma_start(out[c * P : (c + 1) * P, :].rearrange("(c p) v -> p c v", p=P), res[:, c : c + 1, :])
 
         for u in range(2):
             for b in range(2):
                 seen(0, u, b)
                 seen(1, u, b)
-        d_codes = gather(d_tab, user_t[:], U32, "d_codes")
-        third = tile([P, 2, P], F32, "third")
-        scaled(0, 0, low[0][0])
-        scaled(0, 2, third)
-        scaled(1, 0, low[1][0])
-        seen(2, 0, 0)
-        seen(2, 1, 0)
-        scaled(2, 0, low[2][0])
+        d_codes = tile([P, V], U32, "d_codes")
+        nc.vector.tensor_copy(d_codes[:], d_tab[:].bitcast(U32).indirect(user_t[:]))
+
+        second_pair = tile([P, 2, P], F32, "third")
+        open_with(0, 0, low[0][0])
+        open_with(0, 2, second_pair)
+        open_with(1, 0, low[1][0])
+        seen_by_all(2, 0)
+        open_with(2, 0, low[2][0])
         y = [intent(0)]
         y_scaled = [tile([P, 2, P], F32, "y_scaled%d" % u) for u in range(2)]
-        nc.scalar.activation(y_scaled[0][:], y[0][:, :, 0:P], COPY, scale=0.7)
-        seen(3, 0, 0)
-        seen(3, 1, 0)
-        scaled(3, 0, low[3][0])
-        nc.scalar.activation(y_scaled[1][:], y[0][:, :, P:V], COPY, scale=0.7)
+        scale_intent(0)
+        seen_by_all(3, 0)
+        open_with(3, 0, low[3][0])
+        scale_intent(1)
         lower(0, 1, low[0][1], low[0][0])
-        lower(0, 3, low[0][2], third)
+        lower(0, 3, low[0][2], second_pair)
         y.append(intent(1))
-        for c in (3, 2):
-            seen(c, 0, 1)
-            seen(c, 1, 1)
-        next_seen(1, 1)
+        seen_by_all(3, 1)
+        seen_by_all(2, 1)
+
+        step(1, 1)
         nc.vector.tensor_tensor(low[0][3][:], low[0][1][:], low[0][2][:], ALU.min)
-        add_scaled(0)
-        next_seen(1, 2)
-        next_seen(2, 1)
-        next_seen(1, 3)
-        add_scaled(1)
-        next_seen(3, 1)
+        finish_on_gpsimd(0)
+        step(1, 2)
+        step(2, 1)
+        step(1, 3)
+        finish_on_gpsimd(1)
+        step(3, 1)
         for i in range(2, D):
-            next_seen(2, i)
-            next_seen(3, i)
+            step(2, i)
+            step(3, i)
         for c in range(2, 4):
-            score(c, slice(0, V))
-            store(c, c + 1)
+            finish_on_vector(c)

from contextlib import ExitStack

import concourse.mybir as mybir

K, T, S, H, D, V, W, U, G = 1024, 2048, 512, 512, 4, 256, 2048, 1024, 1024
FLOPS = 2 * H * S * (K + V + U)

F32 = mybir.dt.float32
BF16 = mybir.dt.bfloat16
I32 = mybir.dt.int32
U32 = mybir.dt.uint32
U16 = mybir.dt.uint16
U8 = mybir.dt.uint8
FP8X4 = mybir.dt.float8_e4m3fn_x4
ALU = mybir.AluOpType
COPY = mybir.ActivationFunctionType.Copy

P = 128
PACK = 4
BANK = 512
RELEVANCE, REDUNDANCY = 0.7, -0.3

X_ROWS, ED_ROWS = 112, 48
ED_FIRST = 8
X_PIECES = (0, 128, 256, 512)
HALF_CHUNK = 64

Z_BANKS = ((0, 1), (2, 3), (4, 1), (6, 0))
H_BANKS = (4, 5, 6, 4)
Y_BANKS = (5, 7)
CHAINS = {1: (0, 2, 1, 3), 2: (0, 1, 2, 3), 3: (0, 1, 2, 3)}

ALIGN = 256
PAGE = 4096
X1_AT = 0
E_AT = X1_AT + 4 * T
XS_AT = E_AT - T
X0_AT = E_AT + 4 * W
D_AT = X0_AT + 4 * T
DS_AT = D_AT
W_AT = D_AT + 4 * G
H_AT = W_AT + 2 * 4 * PACK * H
PICKED_AT = H_AT + 4 * (S - P) - ALIGN
E1_AT = PICKED_AT + U + V - ALIGN
X_PICKED_AT = E1_AT + 4 * BANK


def tile_picked_ymmr_mmr_p_kernel(
    tc, x_words, x_scales, w1, e_words, e_scales, d_words, d_scales, offs, user, shown, out
):
    nc = tc.nc
    with ExitStack() as ctx:
        keep = ctx.enter_context(tc.tile_pool(name="keep", bufs=1))
        reuse = ctx.enter_context(tc.tile_pool(name="reuse", bufs=1))
        psum = ctx.enter_context(tc.psum_pool(name="psum", bufs=1))

        def bank(shape, name, number):
            return psum.tile(shape, F32, name=name, tag="bank%d" % number)

        def tile(shape, dtype, name, at=None):
            if at is None:
                return keep.tile(shape, dtype, name=name, tag=name, align_bytes=ALIGN)
            return reuse.tile(shape, dtype, name=name, align_bytes=ALIGN if at % PAGE else PAGE, offset=at)

        def load_list(src, name):
            t = keep.tile(list(src.shape), U16, name=name)
            nc.sync.dma_start(t[:], src)
            return t

        def load_words(src, name, at):
            t = tile([P, src.shape[1]], I32, name, at)
            nc.sync.dma_start(t[:], src.rearrange("p n r -> p (n r)").bitcast(I32))
            return t

        def load_w(o):
            nc.sync.dma_start(w_raw[o][:], w1[o * 512 : (o + 1) * 512, :].rearrange("(p j) c -> p j c", j=PACK))

        def move_scale_rows(planes, first, picked, rows):
            for r in range(4):
                src = picked[rows + r : rows + 16 : 4, :]
                nc.sync.dma_start(planes[first + r : P : 32, :].bitcast(I32), src.bitcast(I32))

        def product(acc, lhs, lhs_scales, rhs, rhs_scales, start=True, stop=True):
            nc.tensor.matmul_mx(
                acc, lhsT=lhs.bitcast(FP8X4), lhsT_scale=lhs_scales, rhs=rhs.bitcast(FP8X4), rhs_scale=rhs_scales,
                start=start, stop=stop,
            )

        xs_tab = tile([P, 2 * T], U8, "xs_tab", XS_AT)
        nc.gpsimd.memset(xs_tab[0:X_ROWS, :].bitcast(I32), 0)
        es_tab = tile([P, W], U8, "es_tab")
        ds_tab = tile([P, G], U8, "ds_tab", DS_AT)
        for t in (es_tab, ds_tab):
            nc.vector.memset(t[0:ED_ROWS, :].bitcast(I32), 0)
            nc.vector.memset(t[ED_ROWS + 16 : P, :].bitcast(I32), 0)
        moved = tile([P, 2 * S + U + V], U8, "planes")
        nc.vector.memset(moved[:].bitcast(I32), 0)
        x_moved, ed_moved = moved[:, 0 : 2 * S], moved[:, 2 * S :]
        x_sc = [x_moved[:, 0:S], x_moved[:, S : 2 * S]]
        e_sc = ed_moved[ED_FIRST:P, 0:U]
        d_sc = ed_moved[ED_FIRST:P, U : U + V]

        w_raw = [tile([P, PACK, H], F32, "w_raw%d" % o, W_AT + o * 4 * PACK * H) for o in range(2)]
        nc.sync.dma_start(
            xs_tab[X_ROWS:P, :].bitcast(I32).rearrange("q (o n) -> q o n", o=2),
            x_scales.bitcast(I32).rearrange("o q n -> q o n"),
        )
        offs_t = load_list(offs, "offs_t")
        nc.sync.dma_start(es_tab[ED_ROWS : ED_ROWS + 16, :].bitcast(I32), e_scales[0].bitcast(I32))
        shown_t = load_list(shown, "shown_t")
        load_w(0)
        user_t = load_list(user, "user_t")
        nc.sync.dma_start(ds_tab[ED_ROWS : ED_ROWS + 16, :].bitcast(I32), d_scales[0].bitcast(I32))
        load_w(1)

        x_picked = tile([P, 2 * S], U8, "x_picked", X_PICKED_AT)
        for o in range(2):
            nc.vector.tensor_copy(x_picked[:, o * S : (o + 1) * S], xs_tab[:, o * T : (o + 1) * T].indirect(offs_t[:]))
        ed_picked = tile([P, U + V], U8, "ed_picked", PICKED_AT)
        nc.vector.tensor_copy(
            ed_picked[:, 0:U].rearrange("p (u d v) -> p u v d", u=2, d=D), es_tab[:].indirect(shown_t[:])
        )
        nc.vector.tensor_copy(ed_picked[:, U : U + V], ds_tab[:].indirect(user_t[:]))

        x_tab = [load_words(x_words[0], "x_tab0", X0_AT)]
        move_scale_rows(x_moved, 0, x_picked, X_ROWS)
        x_tab.append(load_words(x_words[1], "x_tab1", X1_AT))
        e_tab = load_words(e_words[0], "e_tab", E_AT)
        move_scale_rows(ed_moved, ED_FIRST, ed_picked, ED_ROWS)
        d_tab = load_words(d_words[0], "d_tab", D_AT)

        def quantise_w(o, scales_at):
            grouped = tile([P, PACK * H], BF16, "w_grouped%d" % o)
            nc.scalar.copy(
                grouped[:].rearrange("p (t m j) -> p m t j", t=PACK, j=PACK),
                w_raw[o][:].rearrange("p j (m t) -> p m t j", t=PACK),
            )
            codes = tile([P, H], U32, "w_codes%d" % o)
            scales = tile([P, H], U8, "w_scales%d" % o, scales_at)
            nc.vector.quantize_mx(codes[:].bitcast(FP8X4), scales[:], grouped[:])
            return codes, scales

        def gather_x(o):
            t = tile([P, S], U32, "x_codes%d" % o)
            for a, b in zip(X_PIECES, X_PIECES[1:]):
                nc.vector.tensor_copy(t[:, a:b], x_tab[o][:].bitcast(U32).indirect(offs_t[:, a // 16 : b // 16]))
            return t

        def gather_seen(u, at):
            t = tile([P, D, P], U32, "e_codes%d" % u, at)
            nc.vector.tensor_copy(
                t[:].rearrange("p d v -> p v d"), e_tab[:].bitcast(U32).indirect(shown_t[:, 32 * u : 32 * (u + 1)])
            )
            return t

        wq = [quantise_w(0, None)]
        x_codes = [gather_x(0)]
        wq.append(quantise_w(1, X_PICKED_AT))
        x_codes.append(gather_x(1))

        h_grouped = [tile([P, 2 * P, PACK], BF16, "h_grouped%d" % pair) for pair in range(2)]
        acc = [bank([P, PACK, P], "acc%d" % c, H_BANKS[c]) for c in range(4)]

        def hidden_pass(c, o):
            cols = slice(c * P, (c + 1) * P)
            for t in range(PACK):
                ch = slice(t * P, (t + 1) * P)
                product(
                    acc[c][:, t, :], wq[o][0][:, ch], wq[o][1][:, ch], x_codes[o][:, cols], x_sc[o][:, cols],
                    start=(o == 0 and t == 0), stop=(o == 1 and t == PACK - 1),
                )

        def round_h(c, a, b):
            at = c % 2 * P
            nc.scalar.copy(h_grouped[c // 2][:, at + a : at + b, :], acc[c][:, :, a:b].rearrange("p t s -> p s t"))

        for c in range(3):
            hidden_pass(c, 0)
        hidden_pass(0, 1)
        round_h(0, 0, HALF_CHUNK)
        round_h(0, HALF_CHUNK, P)
        for c in (1, 2):
            hidden_pass(c, 1)
            round_h(c, 0, P)
        hidden_pass(3, 0)
        hidden_pass(3, 1)
        round_h(3, 0, P)

        h_first = tile([P, P], U32, "h_codes0")
        h_rest = tile([P, S - P], U32, "h_codes1", H_AT)
        h_scales = tile([P, S], U8, "h_scales")
        hq = [(h_first[:], h_scales[:, 0:P])]
        hq.extend((h_rest[:, (c - 1) * P : c * P], h_scales[:, c * P : (c + 1) * P]) for c in range(1, 4))

        def quantise_h(codes, a, b):
            values = h_grouped[a // (2 * P)][:, a % (2 * P) : a % (2 * P) + b - a, :]
            nc.vector.quantize_mx(codes.bitcast(FP8X4), h_scales[:, a:b], values.rearrange("p s t -> p (s t)"))

        quantise_h(h_first[:, 0:HALF_CHUNK], 0, HALF_CHUNK)
        quantise_h(h_first[:, HALF_CHUNK:P], HALF_CHUNK, P)
        e_codes = [gather_seen(0, None)]
        quantise_h(h_rest[:, 0:P], P, 2 * P)
        e_codes.append(gather_seen(1, E1_AT))
        quantise_h(h_rest[:, P : 3 * P], 2 * P, S)

        res = tile([P, 4, V], F32, "res")
        z = [[bank([P, 2, 2, P], "z%d_%d" % (g, b), Z_BANKS[g][b]) for b in range(2)] for g in range(4)]
        low = [[tile([P, 2, P], F32, "low%d_%d" % (g, i)) for i in range(D)] for g in range(4)]

        def seen(c, u, b):
            group, half = (u, c) if c < 2 else (c, u)
            first = u * BANK + b * V
            product(
                z[group][b][:, half, :, :].rearrange("p d v -> p (d v)"), hq[c][0], hq[c][1],
                e_codes[u][:, 2 * b : 2 * b + 2, :].rearrange("p d v -> p (d v)"), e_sc[:, first : first + V],
            )

        def seen_by_all(c, b):
            for u in range(2):
                seen(c, u, b)

        def intent(pair):
            y_pair = bank([P, 2, V], "y%d" % pair, Y_BANKS[pair])
            for i in range(2):
                product(y_pair[:, i, :], hq[2 * pair + i][0], hq[2 * pair + i][1], d_codes[:], d_sc)
            return y_pair

        def open_with(group, item, dst):
            nc.scalar.activation(dst[:], z[group][item // 2][:, :, item % 2, :], COPY, scale=REDUNDANCY)

        def lower(group, item, dst, prior):
            nc.vector.scalar_tensor_tensor(
                dst[:], z[group][item // 2][:, :, item % 2, :], REDUNDANCY, prior[:], ALU.mult, ALU.min
            )

        def step(group, i):
            lower(group, CHAINS[group][i], low[group][i], low[group][i - 1])

        def scale_intent(u):
            nc.scalar.activation(y_scaled[u][:], y[0][:, :, u * P : (u + 1) * P], COPY, scale=RELEVANCE)

        def finish_on_gpsimd(u):
            users = slice(u * P, (u + 1) * P)
            nc.gpsimd.tensor_tensor(res[:, 0:2, users], y_scaled[u][:], low[u][D - 1][:], ALU.add)
            nc.sync.dma_start(out[0 : 2 * P, users].rearrange("(c p) v -> p c v", p=P), res[:, 0:2, users])

        def finish_on_vector(c):
            nearest = low[c][D - 1][:].rearrange("p u v -> p (u v)")
            nc.vector.scalar_tensor_tensor(res[:, c, :], y[1][:, c - 2, :], RELEVANCE, nearest, ALU.mult, ALU.add)
            nc.sync.dma_start(out[c * P : (c + 1) * P, :].rearrange("(c p) v -> p c v", p=P), res[:, c : c + 1, :])

        for u in range(2):
            for b in range(2):
                seen(0, u, b)
                seen(1, u, b)
        d_codes = tile([P, V], U32, "d_codes")
        nc.vector.tensor_copy(d_codes[:], d_tab[:].bitcast(U32).indirect(user_t[:]))

        second_pair = tile([P, 2, P], F32, "third")
        open_with(0, 0, low[0][0])
        open_with(0, 2, second_pair)
        open_with(1, 0, low[1][0])
        seen_by_all(2, 0)
        open_with(2, 0, low[2][0])
        y = [intent(0)]
        y_scaled = [tile([P, 2, P], F32, "y_scaled%d" % u) for u in range(2)]
        scale_intent(0)
        seen_by_all(3, 0)
        open_with(3, 0, low[3][0])
        scale_intent(1)
        lower(0, 1, low[0][1], low[0][0])
        lower(0, 3, low[0][2], second_pair)
        y.append(intent(1))
        seen_by_all(3, 1)
        seen_by_all(2, 1)

        step(1, 1)
        nc.vector.tensor_tensor(low[0][3][:], low[0][1][:], low[0][2][:], ALU.min)
        finish_on_gpsimd(0)
        step(1, 2)
        step(2, 1)
        step(1, 3)
        finish_on_gpsimd(1)
        step(3, 1)
        for i in range(2, D):
            step(2, i)
            step(3, i)
        for c in range(2, 4):
            finish_on_vector(c)
